import numpy as np
import ml_dtypes


def mxq(x, axis, fmt="e4m3"):
    dtype, down = {"e4m3": (ml_dtypes.float8_e4m3fn, 7), "e5m2": (ml_dtypes.float8_e5m2, 14)}[fmt]
    v = np.moveaxis(np.asarray(x, np.float32).astype(ml_dtypes.bfloat16).astype(np.float64), axis, -1)
    blocks = v.reshape(v.shape[:-1] + (-1, 32))
    amax = np.abs(blocks).max(-1, keepdims=True)
    byte = np.maximum(np.where(amax > 0, np.frexp(amax)[1] - 1 + 127, 0) - down, 1)
    scale = np.exp2(byte - 127.0)
    codes = (blocks / scale).astype(np.float32).astype(dtype).astype(np.float64)
    return np.moveaxis((codes * scale).reshape(v.shape), -1, axis)


WIDE = False


def mx_kscale(k):
    if not WIDE:
        return np.ones(k)
    levels = np.array([10, -10, 5, -5, 0])
    if k % 512:
        return np.exp2(np.random.permutation(np.resize(levels, k // 32))).repeat(32)
    a = np.empty((k // 512, 16))
    for p in range(k // 512):
        a[p, :8] = np.random.permutation(np.resize(levels, 8))
        for g in range(8):
            far = levels[np.abs(levels - a[p, g]) >= 10]
            a[p, g + 8] = far[np.random.randint(len(far))]
    return np.exp2(a.ravel()).repeat(32)


def f64(x):
    return np.asarray(x).astype(np.float64)


def striped(idx):
    return np.tile(np.asarray(idx).reshape(-1, 16).T, (8, 1)).astype(np.uint16)


def unstriped(offs):
    return offs[:16].T.reshape(-1).astype(np.int64)


E2M1 = np.array([0.0, 0.5, 1.0, 1.5, 2.0, 3.0, 4.0, 6.0, -0.0, -0.5, -1.0, -1.5, -2.0, -3.0, -4.0, -6.0])


def pack_weight(w, fmt):
    k, n = w.shape
    w = f64(np.asarray(w, np.float32).astype(ml_dtypes.bfloat16)).reshape(k // 32, 32, n)
    amax = np.abs(w).max(1)
    if fmt == "e4m3":
        byte = np.frexp(amax)[1] - 1 + 127 - 7
    else:
        mant, ex = np.frexp(amax / 6.0)
        byte = np.where(mant > 0.5, ex, ex - 1) + 127
    byte = np.clip(np.where(amax > 0, byte, 1), 1, 254)
    scaled = (w * np.exp2(127.0 - byte)[:, None, :]).reshape(k, n).astype(np.float32)
    by_word = np.ascontiguousarray(scaled.reshape(k // 512, 128, 4, n).transpose(0, 1, 3, 2))
    if fmt == "e4m3":
        words = by_word.astype(ml_dtypes.float8_e4m3fn).view(np.uint8)
    else:
        c = by_word.astype(ml_dtypes.float4_e2m1fn).view(np.uint8) & 0xF
        words = (c[..., 0::2] | (c[..., 1::2] << 4)).reshape(k // 512, 128, 2 * n)
    return np.ascontiguousarray(words), np.ascontiguousarray(byte.astype(np.uint8).reshape(k // 512, 16, n))


def unpack_weight(words, scales, fmt):
    g, _, n = scales.shape
    words = np.ascontiguousarray(words).reshape(g, 128, n, -1)
    if fmt == "e4m3":
        vals = words.view(ml_dtypes.float8_e4m3fn).astype(np.float64)
    else:
        nib = np.empty((g, 128, n, 4), np.uint8)
        nib[..., 0::2] = words & 0xF
        nib[..., 1::2] = words >> 4
        vals = E2M1[nib]
    vals = vals * np.repeat(np.exp2(scales.astype(np.float64) - 127.0), 8, axis=1)[..., None]
    return vals.transpose(0, 1, 3, 2).reshape(g * 512, n)


D, T, I, M, E = 512, 2048, 512, 128, 512


def setup_inputs():
    n = np.random.standard_normal
    idx = np.random.permutation(T)[:I]
    fd = mx_kscale(D)
    fi = mx_kscale(I)
    ti = np.ones(T)
    ti[idx] = fi
    ptsp = pack_weight(n((D, T)) / fd[:, None], "e2m1")
    return {
        "pts_words": ptsp[0],
        "pts_scales": ptsp[1],
        "cent": (n((D, M)) * 0.5 / np.sqrt(D) * fd[:, None]).astype(np.float32),
        "fac": (np.random.uniform(0.5, 2.0, (I, 1)) * fi[:, None]).astype(np.float32),
        "vals": (n((E, T)) / ti).astype(np.float32),
        "offs": striped(idx),
    }


def reference(pts_words, pts_scales, cent, fac, vals, offs):
    idx = unstriped(offs)
    ptsu = unpack_weight(pts_words, pts_scales, "e2m1")
    ptsidxg = ptsu[:, idx]
    centq = mxq(f64(cent), 0, "e4m3")
    a = ptsidxg.T @ centq
    p = np.exp(a - np.max(a, axis=1, keepdims=True))
    r = p / np.sum(p, axis=1, keepdims=True)
    w = r * f64(fac)
    vt = f64(vals)[:, idx].T
    wq = mxq(w, 0, "e4m3")
    vtq = mxq(vt, 0, "e4m3")
    z = wq.T @ vtq
    rt = r.T
    y = z / np.sum(rt, axis=1, keepdims=True)
    return y

@@ -1,0 +1,172 @@
+from contextlib import ExitStack
+
+import concourse.mybir as mybir
+from concourse.masks import make_identity
+
+D, T, I, M, E = 512, 2048, 512, 128, 512
+FLOPS = 2 * I * D * M + 2 * M * I * E
+
+F32 = mybir.dt.float32
+BF16 = mybir.dt.bfloat16
+I32 = mybir.dt.int32
+U32 = mybir.dt.uint32
+U16 = mybir.dt.uint16
+U8 = mybir.dt.uint8
+FP8X4 = mybir.dt.float8_e4m3fn_x4
+FP4X4 = mybir.dt.float4_e2m1fn_x4
+ALU = mybir.AluOpType
+ACT = mybir.ActivationFunctionType
+AXIS = mybir.AxisListType
+
+P = 128
+PACK = 4
+BLOCKS = E // P
+
+
+def tile_attend_clustermeans_kernel(tc, pts_words, pts_scales, cent, fac, vals, offs, out):
+    nc = tc.nc
+    with ExitStack() as ctx:
+        sb = ctx.enter_context(tc.tile_pool(name="sb", bufs=1))
+        ps = ctx.enter_context(tc.psum_pool(name="ps", bufs=1))
+
+        offsets = sb.tile([P, I // 16], U16, name="offsets")
+        nc.sync.dma_start(offsets[:], offs)
+
+        byte_pool = sb.tile([P, T], U8, name="byte_pool", align_bytes=64)
+        nc.gpsimd.memset(byte_pool[:].bitcast(I32), 0)
+        for q in range(4):
+            nc.scalar.dma_start(
+                byte_pool[32 * q : 32 * q + 4, :].bitcast(I32),
+                pts_scales[0, 4 * q : 4 * q + 4, :].bitcast(I32),
+            )
+        word_pool = sb.tile([P, T], U16, name="word_pool", align_bytes=64)
+        nc.sync.dma_start(word_pool[:].bitcast(I32), pts_words[0].bitcast(I32))
+        cent_raw = sb.tile([P, PACK, M], F32, name="cent_raw")
+        nc.sync.dma_start(cent_raw[:], cent.rearrange("(p t) m -> p t m", t=PACK))
+        val_pool = []
+        for b in range(BLOCKS):
+            tile_b = sb.tile([P, T], F32, name="val_pool%d" % b, tag="big%d" % b, align_bytes=64)
+            nc.sync.dma_start(tile_b[:], vals[b * P : (b + 1) * P, :])
+            val_pool.append(tile_b)
+        ident = sb.tile([P, P], F32, name="ident")
+        make_identity(nc, ident[:])
+        fac_sb = sb.tile([P, PACK], F32, name="fac_sb")
+        nc.gpsimd.dma_start(fac_sb[:], fac.rearrange("(p t) o -> p (t o)", t=PACK))
+
+
+        word_list = sb.tile([P, I], U16, name="word_list", align_bytes=64)
+        nc.vector.tensor_copy(word_list[:], word_pool[:].indirect(offsets[:]))
+        byte_list = sb.tile([P, I], U8, name="byte_list", align_bytes=64)
+        nc.vector.tensor_copy(byte_list[:], byte_pool[:].indirect(offsets[:]))
+        word_dealt = sb.tile([P, PACK, P], U16, name="word_dealt", align_bytes=64)
+        nc.vector.tensor_copy(word_dealt[:], word_list[:].rearrange("p (s t) -> p t s", t=PACK))
+        byte_dealt = sb.tile([P, PACK, P], U8, name="byte_dealt", align_bytes=64)
+        nc.vector.tensor_copy(byte_dealt[:], byte_list[:].rearrange("p (s t) -> p t s", t=PACK))
+
+        cent_bf = sb.tile([P, M, PACK], BF16, name="cent_bf", align_bytes=64)
+        nc.scalar.copy(cent_bf[:], cent_raw[:].rearrange("p t m -> p m t"))
+        cent_codes = sb.tile([P, M], U32, name="cent_codes", align_bytes=64)
+        cent_bytes = sb.tile([P, M], U8, name="cent_bytes", align_bytes=64)
+        nc.vector.quantize_mx(
+            out=cent_codes[:].bitcast(FP8X4),
+            scales=cent_bytes[:],
+            in_=cent_bf[:].rearrange("p m t -> p (m t)"),
+        )
+
+        scores = ps.tile([P, PACK, M], F32, name="scores")
+        for t in range(PACK):
+            nc.tensor.matmul_mx(
+                out=scores[:, t, :],
+                lhsT=word_dealt[:, t, :].bitcast(FP4X4),
+                lhsT_scale=byte_dealt[:, t, :],
+                rhs=cent_codes[:].bitcast(FP8X4),
+                rhs_scale=cent_bytes[:],
+                start=True,
+                stop=True,
+            )
+
+        neg_max = sb.tile([P, PACK], F32, name="neg_max")
+        nc.vector.tensor_reduce(neg_max[:], scores[:], axis=AXIS.X, op=ALU.max, negate=True)
+        expd = sb.tile([P, PACK, M], F32, name="expd")
+        row_sum = sb.tile([P, PACK], F32, name="row_sum")
+        for t in range(PACK):
+            nc.scalar.activation(
+                expd[:, t, :], scores[:, t, :], ACT.Exp,
+                bias=neg_max[:, t : t + 1], accum_out=row_sum[:, t : t + 1],
+            )
+        row_inv = sb.tile([P, PACK], F32, name="row_inv")
+        nc.vector.reciprocal(row_inv[:], row_sum[:])
+        share = sb.tile([P, PACK, M], F32, name="share")
+        for t in range(PACK):
+            nc.scalar.activation(share[:, t, :], expd[:, t, :], ACT.Copy, scale=row_inv[:, t : t + 1])
+        w_bf = sb.tile([P, M, PACK], BF16, name="w_bf", align_bytes=64)
+        nc.vector.tensor_tensor(
+            w_bf[:],
+            share[:].rearrange("p t m -> p m t"),
+            fac_sb[:].unsqueeze(1).to_broadcast([P, M, PACK]),
+            ALU.mult,
+        )
+        w_codes = sb.tile([P, M], U32, name="w_codes", align_bytes=64)
+        w_bytes = sb.tile([P, M], U8, name="w_bytes", align_bytes=64)
+        nc.vector.quantize_mx(
+            out=w_codes[:].bitcast(FP8X4),
+            scales=w_bytes[:],
+            in_=w_bf[:].rearrange("p m t -> p (m t)"),
+        )
+
+        share_t = ps.tile([P, P], F32, name="share_t")
+        for t in range(PACK):
+            nc.tensor.matmul(
+                share_t[:], share[:, t, :], ident[:],
+                start=(t == 0), stop=(t == PACK - 1), is_transpose=True,
+            )
+        col_sum = sb.tile([P, 1], F32, name="col_sum")
+        nc.vector.tensor_reduce(col_sum[:], share_t[:], axis=AXIS.X, op=ALU.add)
+        col_inv = sb.tile([P, 1], F32, name="col_inv")
+        nc.vector.reciprocal(col_inv[:], col_sum[:])
+
+        z_head = ps.tile([P, (BLOCKS - 1) * P], F32, name="z_head")
+        z_last = ps.tile([P, P], F32, name="z_last")
+        v_bf = []
+
+        def gather_and_turn(b):
+            listed = sb.tile([P, I], BF16, name="listed%d" % b, align_bytes=64)
+            nc.vector.tensor_copy(listed[:], val_pool[b][:].indirect(offsets[:]))
+            pairs = listed[:].bitcast(F32)
+            turned = ps.tile([P, 2, P], F32, name="turned%d" % b)
+            for u in range(2):
+                nc.tensor.transpose(turned[:, u, :], pairs[:, u : 2 * P : 2], ident[:])
+            rows = sb.tile([P, P * PACK], BF16, name="v_bf%d" % b, align_bytes=64)
+            nc.scalar.copy(
+                rows[:].bitcast(F32).rearrange("p (e u) -> p e u", u=2),
+                turned[:].rearrange("p u e -> p e u"),
+            )
+            v_bf.append(rows)
+
+        def multiply(b):
+            v_codes = sb.tile([P, P], U32, name="v_codes%d" % b, tag="big%d" % ((b + 1) % BLOCKS) if b < BLOCKS - 1 else "last", align_bytes=64)
+            v_bytes = sb.tile([P, P], U8, name="v_bytes%d" % b, align_bytes=64)
+            nc.vector.quantize_mx(out=v_codes[:].bitcast(FP8X4), scales=v_bytes[:], in_=v_bf[b][:])
+            z = z_last[:] if b == BLOCKS - 1 else z_head[:, b * P : (b + 1) * P]
+            nc.tensor.matmul_mx(
+                out=z,
+                lhsT=w_codes[:].bitcast(FP8X4),
+                lhsT_scale=w_bytes[:],
+                rhs=v_codes[:].bitcast(FP8X4),
+                rhs_scale=v_bytes[:],
+                start=True,
+                stop=True,
+            )
+
+        def store(bank, first, width):
+            mean = sb.tile([P, width], F32, name="mean%d" % first)
+            nc.scalar.activation(mean[:], bank[:], ACT.Copy, scale=col_inv[:])
+            nc.sync.dma_start(out[:, first : first + width], mean[:])
+
+        gather_and_turn(0)
+        for b in range(1, BLOCKS):
+            gather_and_turn(b)
+            multiply(b - 1)
+        store(z_head, 0, (BLOCKS - 1) * P)
+        multiply(BLOCKS - 1)
+        store(z_last, (BLOCKS - 1) * P, P)

@@ -33,9 +33,9 @@ def tile_attend_clustermeans_kernel(tc, pts_words, pts_scales, cent, fac, vals, 
         nc.sync.dma_start(offsets[:], offs)
 
         byte_pool = sb.tile([P, T], U8, name="byte_pool", align_bytes=64)
-        nc.gpsimd.memset(byte_pool[:].bitcast(I32), 0)
+        nc.vector.memset(byte_pool[:].bitcast(I32), 0)
         for q in range(4):
-            nc.scalar.dma_start(
+            nc.sync.dma_start(
                 byte_pool[32 * q : 32 * q + 4, :].bitcast(I32),
                 pts_scales[0, 4 * q : 4 * q + 4, :].bitcast(I32),
             )
@@ -54,24 +54,24 @@ def tile_attend_clustermeans_kernel(tc, pts_words, pts_scales, cent, fac, vals, 
         nc.gpsimd.dma_start(fac_sb[:], fac.rearrange("(p t) o -> p (t o)", t=PACK))
 
 
-        word_list = sb.tile([P, I], U16, name="word_list", align_bytes=64)
-        nc.vector.tensor_copy(word_list[:], word_pool[:].indirect(offsets[:]))
         byte_list = sb.tile([P, I], U8, name="byte_list", align_bytes=64)
         nc.vector.tensor_copy(byte_list[:], byte_pool[:].indirect(offsets[:]))
-        word_dealt = sb.tile([P, PACK, P], U16, name="word_dealt", align_bytes=64)
-        nc.vector.tensor_copy(word_dealt[:], word_list[:].rearrange("p (s t) -> p t s", t=PACK))
+        word_list = sb.tile([P, I], U16, name="word_list", align_bytes=64)
+        nc.vector.tensor_copy(word_list[:], word_pool[:].indirect(offsets[:]))
         byte_dealt = sb.tile([P, PACK, P], U8, name="byte_dealt", align_bytes=64)
         nc.vector.tensor_copy(byte_dealt[:], byte_list[:].rearrange("p (s t) -> p t s", t=PACK))
+        word_dealt = sb.tile([P, PACK, P], U16, name="word_dealt", align_bytes=64)
+        nc.vector.tensor_copy(word_dealt[:], word_list[:].rearrange("p (s t) -> p t s", t=PACK))
+
+        def quantise(name, rows, width, tag):
+            codes = sb.tile([P, width], U32, name=name + "_codes", tag=tag, align_bytes=64)
+            plane = sb.tile([P, width], U8, name=name + "_bytes", align_bytes=64)
+            nc.vector.quantize_mx(out=codes[:].bitcast(FP8X4), scales=plane[:], in_=rows)
+            return codes, plane
 
         cent_bf = sb.tile([P, M, PACK], BF16, name="cent_bf", align_bytes=64)
         nc.scalar.copy(cent_bf[:], cent_raw[:].rearrange("p t m -> p m t"))
-        cent_codes = sb.tile([P, M], U32, name="cent_codes", align_bytes=64)
-        cent_bytes = sb.tile([P, M], U8, name="cent_bytes", align_bytes=64)
-        nc.vector.quantize_mx(
-            out=cent_codes[:].bitcast(FP8X4),
-            scales=cent_bytes[:],
-            in_=cent_bf[:].rearrange("p m t -> p (m t)"),
-        )
+        cent_mx = quantise("cent", cent_bf[:].rearrange("p m t -> p (m t)"), M, "cent_codes")
 
         scores = ps.tile([P, PACK, M], F32, name="scores")
         for t in range(PACK):
@@ -79,13 +79,43 @@ def tile_attend_clustermeans_kernel(tc, pts_words, pts_scales, cent, fac, vals, 
                 out=scores[:, t, :],
                 lhsT=word_dealt[:, t, :].bitcast(FP4X4),
                 lhsT_scale=byte_dealt[:, t, :],
-                rhs=cent_codes[:].bitcast(FP8X4),
-                rhs_scale=cent_bytes[:],
+                rhs=cent_mx[0][:].bitcast(FP8X4),
+                rhs_scale=cent_mx[1][:],
                 start=True,
                 stop=True,
             )
 
-        neg_max = sb.tile([P, PACK], F32, name="neg_max")
+        seen = []
+
+        def gather_and_turn(b):
+            listed = sb.tile([P, I], BF16, name="listed%d" % b, align_bytes=64)
+            nc.vector.tensor_copy(listed[:], val_pool[b][:].indirect(offsets[:]))
+            seen.append(listed)
+            pairs = listed[:].bitcast(F32)
+            turned = ps.tile([P, 2, P], F32, name="turned%d" % b, tag="turned%d" % (b % 3))
+            for u in range(2):
+                nc.tensor.transpose(turned[:, u, :], pairs[:, u : 2 * P : 2], ident[:])
+            return turned
+
+        def weave(turned, rows):
+            nc.scalar.copy(
+                rows.bitcast(F32).rearrange("p (e u) -> p e u", u=2),
+                turned[:].rearrange("p u e -> p e u"),
+            )
+
+        def multiply(z, moving, first):
+            nc.tensor.matmul_mx(
+                out=z,
+                lhsT=w0_mx[0][:, :M].bitcast(FP8X4),
+                lhsT_scale=w0_mx[1][:, :M],
+                rhs=moving[0][:, first:].bitcast(FP8X4),
+                rhs_scale=moving[1][:, first:],
+                start=True,
+                stop=True,
+            )
+
+        turned0 = gather_and_turn(0)
+        neg_max = sb.tile([P, PACK], F32, name="neg_max", tag="big0", align_bytes=64)
         nc.vector.tensor_reduce(neg_max[:], scores[:], axis=AXIS.X, op=ALU.max, negate=True)
         expd = sb.tile([P, PACK, M], F32, name="expd")
         row_sum = sb.tile([P, PACK], F32, name="row_sum")
@@ -94,79 +124,48 @@ def tile_attend_clustermeans_kernel(tc, pts_words, pts_scales, cent, fac, vals, 
                 expd[:, t, :], scores[:, t, :], ACT.Exp,
                 bias=neg_max[:, t : t + 1], accum_out=row_sum[:, t : t + 1],
             )
-        row_inv = sb.tile([P, PACK], F32, name="row_inv")
+        rows12 = sb.tile([P, 2 * I], BF16, name="rows12", tag="rows12", align_bytes=64)
+        weave(gather_and_turn(1), rows12[:, :I])
+        row_inv = sb.tile([P, PACK], F32, name="row_inv", tag="big1", align_bytes=64)
         nc.vector.reciprocal(row_inv[:], row_sum[:])
         share = sb.tile([P, PACK, M], F32, name="share")
         for t in range(PACK):
             nc.scalar.activation(share[:, t, :], expd[:, t, :], ACT.Copy, scale=row_inv[:, t : t + 1])
-        w_bf = sb.tile([P, M, PACK], BF16, name="w_bf", align_bytes=64)
-        nc.vector.tensor_tensor(
-            w_bf[:],
-            share[:].rearrange("p t m -> p m t"),
-            fac_sb[:].unsqueeze(1).to_broadcast([P, M, PACK]),
-            ALU.mult,
-        )
-        w_codes = sb.tile([P, M], U32, name="w_codes", align_bytes=64)
-        w_bytes = sb.tile([P, M], U8, name="w_bytes", align_bytes=64)
-        nc.vector.quantize_mx(
-            out=w_codes[:].bitcast(FP8X4),
-            scales=w_bytes[:],
-            in_=w_bf[:].rearrange("p m t -> p (m t)"),
-        )
-
         share_t = ps.tile([P, P], F32, name="share_t")
         for t in range(PACK):
             nc.tensor.matmul(
                 share_t[:], share[:, t, :], ident[:],
                 start=(t == 0), stop=(t == PACK - 1), is_transpose=True,
             )
+        share_sb = sb.tile([P, P], F32, name="share_sb")
         col_sum = sb.tile([P, 1], F32, name="col_sum")
-        nc.vector.tensor_reduce(col_sum[:], share_t[:], axis=AXIS.X, op=ALU.add)
-        col_inv = sb.tile([P, 1], F32, name="col_inv")
+        nc.scalar.activation(share_sb[:], share_t[:], ACT.Copy, accum_out=col_sum[:])
+
+        turned2 = gather_and_turn(2)
+        rows_w0 = sb.tile([P, 2 * I], BF16, name="rows_w0", tag="big2", align_bytes=64)
+        weave(turned0, rows_w0[:, I:])
+        weave(turned2, rows12[:, I:])
+        nc.vector.tensor_tensor(
+            rows_w0[:, :I].rearrange("p (m t) -> p m t", t=PACK),
+            share[:].rearrange("p t m -> p m t"),
+            fac_sb[:].unsqueeze(1).to_broadcast([P, M, PACK]),
+            ALU.mult,
+        )
+        rows3 = sb.tile([P, I], BF16, name="rows3", tag="rows3", align_bytes=64)
+        weave(gather_and_turn(3), rows3[:])
+        w0_mx = quantise("w0", rows_w0[:], 2 * P, "big3")
+        v12 = quantise("v12", rows12[:], 2 * P, "big2")
+        col_inv = sb.tile([P, 1], F32, name="col_inv", tag="rows12", align_bytes=64)
         nc.vector.reciprocal(col_inv[:], col_sum[:])
-
-        z_head = ps.tile([P, (BLOCKS - 1) * P], F32, name="z_head")
-        z_last = ps.tile([P, P], F32, name="z_last")
-        v_bf = []
-
-        def gather_and_turn(b):
-            listed = sb.tile([P, I], BF16, name="listed%d" % b, align_bytes=64)
-            nc.vector.tensor_copy(listed[:], val_pool[b][:].indirect(offsets[:]))
-            pairs = listed[:].bitcast(F32)
-            turned = ps.tile([P, 2, P], F32, name="turned%d" % b)
-            for u in range(2):
-                nc.tensor.transpose(turned[:, u, :], pairs[:, u : 2 * P : 2], ident[:])
-            rows = sb.tile([P, P * PACK], BF16, name="v_bf%d" % b, align_bytes=64)
-            nc.scalar.copy(
-                rows[:].bitcast(F32).rearrange("p (e u) -> p e u", u=2),
-                turned[:].rearrange("p u e -> p e u"),
-            )
-            v_bf.append(rows)
-
-        def multiply(b):
-            v_codes = sb.tile([P, P], U32, name="v_codes%d" % b, tag="big%d" % ((b + 1) % BLOCKS) if b < BLOCKS - 1 else "last", align_bytes=64)
-            v_bytes = sb.tile([P, P], U8, name="v_bytes%d" % b, align_bytes=64)
-            nc.vector.quantize_mx(out=v_codes[:].bitcast(FP8X4), scales=v_bytes[:], in_=v_bf[b][:])
-            z = z_last[:] if b == BLOCKS - 1 else z_head[:, b * P : (b + 1) * P]
-            nc.tensor.matmul_mx(
-                out=z,
-                lhsT=w_codes[:].bitcast(FP8X4),
-                lhsT_scale=w_bytes[:],
-                rhs=v_codes[:].bitcast(FP8X4),
-                rhs_scale=v_bytes[:],
-                start=True,
-                stop=True,
-            )
-
-        def store(bank, first, width):
-            mean = sb.tile([P, width], F32, name="mean%d" % first)
-            nc.scalar.activation(mean[:], bank[:], ACT.Copy, scale=col_inv[:])
-            nc.sync.dma_start(out[:, first : first + width], mean[:])
-
-        gather_and_turn(0)
-        for b in range(1, BLOCKS):
-            gather_and_turn(b)
-            multiply(b - 1)
-        store(z_head, 0, (BLOCKS - 1) * P)
-        multiply(BLOCKS - 1)
-        store(z_last, (BLOCKS - 1) * P, P)
+        v3 = quantise("v3", rows3[:], P, "v3_codes")
+        z012 = ps.tile([P, 3 * P], F32, name="z012")
+        z3 = ps.tile([P, P], F32, name="z3")
+        multiply(z012[:, :P], w0_mx, M)
+        multiply(z012[:, P:], v12, 0)
+        multiply(z3[:], v3, 0)
+        mean012 = sb.tile([P, 3 * P], F32, name="mean012")
+        nc.scalar.activation(mean012[:], z012[:], ACT.Copy, scale=col_inv[:])
+        nc.sync.dma_start(out[:, : 3 * P], mean012[:])
+        mean3 = sb.tile([P, P], F32, name="mean3")
+        nc.vector.tensor_scalar(mean3[:], z3[:], col_inv[:], None, ALU.mult)
+        nc.sync.dma_start(out[:, 3 * P :], mean3[:])

@@ -1,7 +1,6 @@
 from contextlib import ExitStack
 
 import concourse.mybir as mybir
-from concourse.masks import make_identity
 
 D, T, I, M, E = 512, 2048, 512, 128, 512
 FLOPS = 2 * I * D * M + 2 * M * I * E
@@ -21,16 +20,22 @@ AXIS = mybir.AxisListType
 P = 128
 PACK = 4
 BLOCKS = E // P
+ROW = 4 * T
 
 
 def tile_attend_clustermeans_kernel(tc, pts_words, pts_scales, cent, fac, vals, offs, out):
     nc = tc.nc
     with ExitStack() as ctx:
         sb = ctx.enter_context(tc.tile_pool(name="sb", bufs=1))
+        big = ctx.enter_context(tc.tile_pool(name="big", bufs=1))
         ps = ctx.enter_context(tc.psum_pool(name="ps", bufs=1))
 
         offsets = sb.tile([P, I // 16], U16, name="offsets")
+        word_pool = sb.tile([P, T], U16, name="word_pool", align_bytes=64)
+        nc.sync.dma_start(word_pool[:].bitcast(I32), pts_words[0].bitcast(I32))
         nc.sync.dma_start(offsets[:], offs)
+        cent_raw = sb.tile([P, PACK, M], F32, name="cent_raw")
+        nc.sync.dma_start(cent_raw[:], cent.rearrange("(p t) m -> p t m", t=PACK))
 
         byte_pool = sb.tile([P, T], U8, name="byte_pool", align_bytes=64)
         nc.vector.memset(byte_pool[:].bitcast(I32), 0)
@@ -39,39 +44,42 @@ def tile_attend_clustermeans_kernel(tc, pts_words, pts_scales, cent, fac, vals, 
                 byte_pool[32 * q : 32 * q + 4, :].bitcast(I32),
                 pts_scales[0, 4 * q : 4 * q + 4, :].bitcast(I32),
             )
-        word_pool = sb.tile([P, T], U16, name="word_pool", align_bytes=64)
-        nc.sync.dma_start(word_pool[:].bitcast(I32), pts_words[0].bitcast(I32))
-        cent_raw = sb.tile([P, PACK, M], F32, name="cent_raw")
-        nc.sync.dma_start(cent_raw[:], cent.rearrange("(p t) m -> p t m", t=PACK))
+        zeros = big.tile([P, BLOCKS * T], F32, name="zeros", offset=0, align_bytes=64)
+        nc.gpsimd.memset(zeros[:, :P], 0.0)
+        ident = sb.tile([P, P], F32, name="ident")
+        nc.gpsimd.affine_select(
+            out=ident[:], in_=zeros[:, :P], compare_op=ALU.not_equal, fill=1.0,
+            base=0, pattern=[[-1, P]], channel_multiplier=1,
+        )
         val_pool = []
         for b in range(BLOCKS):
-            tile_b = sb.tile([P, T], F32, name="val_pool%d" % b, tag="big%d" % b, align_bytes=64)
+            tile_b = big.tile([P, T], F32, name="val_pool%d" % b, offset=b * ROW, align_bytes=64)
             nc.sync.dma_start(tile_b[:], vals[b * P : (b + 1) * P, :])
             val_pool.append(tile_b)
-        ident = sb.tile([P, P], F32, name="ident")
-        make_identity(nc, ident[:])
         fac_sb = sb.tile([P, PACK], F32, name="fac_sb")
         nc.gpsimd.dma_start(fac_sb[:], fac.rearrange("(p t) o -> p (t o)", t=PACK))
 
-
-        byte_list = sb.tile([P, I], U8, name="byte_list", align_bytes=64)
-        nc.vector.tensor_copy(byte_list[:], byte_pool[:].indirect(offsets[:]))
         word_list = sb.tile([P, I], U16, name="word_list", align_bytes=64)
         nc.vector.tensor_copy(word_list[:], word_pool[:].indirect(offsets[:]))
-        byte_dealt = sb.tile([P, PACK, P], U8, name="byte_dealt", align_bytes=64)
-        nc.vector.tensor_copy(byte_dealt[:], byte_list[:].rearrange("p (s t) -> p t s", t=PACK))
         word_dealt = sb.tile([P, PACK, P], U16, name="word_dealt", align_bytes=64)
         nc.vector.tensor_copy(word_dealt[:], word_list[:].rearrange("p (s t) -> p t s", t=PACK))
+        byte_list = sb.tile([P, I], U8, name="byte_list", align_bytes=64)
+        nc.vector.tensor_copy(byte_list[:], byte_pool[:].indirect(offsets[:]))
+        byte_dealt = sb.tile([P, PACK, P], U8, name="byte_dealt", align_bytes=64)
+        nc.vector.tensor_copy(byte_dealt[:], byte_list[:].rearrange("p (s t) -> p t s", t=PACK))
 
-        def quantise(name, rows, width, tag):
-            codes = sb.tile([P, width], U32, name=name + "_codes", tag=tag, align_bytes=64)
-            plane = sb.tile([P, width], U8, name=name + "_bytes", align_bytes=64)
+        def quantise(name, rows, codes):
+            plane = sb.tile([P, codes.shape[1]], U8, name=name + "_bytes", align_bytes=64)
             nc.vector.quantize_mx(out=codes[:].bitcast(FP8X4), scales=plane[:], in_=rows)
             return codes, plane
 
+        def behind(b, at, shape, dtype, name):
+            return big.tile(shape, dtype, name=name, offset=b * ROW + at, align_bytes=64)
+
         cent_bf = sb.tile([P, M, PACK], BF16, name="cent_bf", align_bytes=64)
         nc.scalar.copy(cent_bf[:], cent_raw[:].rearrange("p t m -> p m t"))
-        cent_mx = quantise("cent", cent_bf[:].rearrange("p m t -> p (m t)"), M, "cent_codes")
+        cent_codes = sb.tile([P, M], U32, name="cent_codes", align_bytes=64)
+        cent_mx = quantise("cent", cent_bf[:].rearrange("p m t -> p (m t)"), cent_codes)
 
         scores = ps.tile([P, PACK, M], F32, name="scores")
         for t in range(PACK):
@@ -103,19 +111,23 @@ def tile_attend_clustermeans_kernel(tc, pts_words, pts_scales, cent, fac, vals, 
                 turned[:].rearrange("p u e -> p e u"),
             )
 
-        def multiply(z, moving, first):
+        def multiply(z, weights, moving, first):
             nc.tensor.matmul_mx(
                 out=z,
-                lhsT=w0_mx[0][:, :M].bitcast(FP8X4),
-                lhsT_scale=w0_mx[1][:, :M],
+                lhsT=weights[0][:, :M].bitcast(FP8X4),
+                lhsT_scale=weights[1][:, :M],
                 rhs=moving[0][:, first:].bitcast(FP8X4),
                 rhs_scale=moving[1][:, first:],
                 start=True,
                 stop=True,
             )
 
+        rows01 = sb.tile([P, 2 * I], BF16, name="rows01", align_bytes=64)
+        rows_w2 = sb.tile([P, 2 * I], BF16, name="rows_w2", align_bytes=64)
+        rows3 = sb.tile([P, I], BF16, name="rows3", align_bytes=64)
+
         turned0 = gather_and_turn(0)
-        neg_max = sb.tile([P, PACK], F32, name="neg_max", tag="big0", align_bytes=64)
+        neg_max = behind(0, 0, [P, PACK], F32, "neg_max")
         nc.vector.tensor_reduce(neg_max[:], scores[:], axis=AXIS.X, op=ALU.max, negate=True)
         expd = sb.tile([P, PACK, M], F32, name="expd")
         row_sum = sb.tile([P, PACK], F32, name="row_sum")
@@ -124,48 +136,48 @@ def tile_attend_clustermeans_kernel(tc, pts_words, pts_scales, cent, fac, vals, 
                 expd[:, t, :], scores[:, t, :], ACT.Exp,
                 bias=neg_max[:, t : t + 1], accum_out=row_sum[:, t : t + 1],
             )
-        rows12 = sb.tile([P, 2 * I], BF16, name="rows12", tag="rows12", align_bytes=64)
-        weave(gather_and_turn(1), rows12[:, :I])
-        row_inv = sb.tile([P, PACK], F32, name="row_inv", tag="big1", align_bytes=64)
+        weave(turned0, rows01[:, :I])
+        turned1 = gather_and_turn(1)
+        row_inv = behind(1, 0, [P, PACK], F32, "row_inv")
         nc.vector.reciprocal(row_inv[:], row_sum[:])
         share = sb.tile([P, PACK, M], F32, name="share")
         for t in range(PACK):
             nc.scalar.activation(share[:, t, :], expd[:, t, :], ACT.Copy, scale=row_inv[:, t : t + 1])
+        weave(turned1, rows01[:, I:])
         share_t = ps.tile([P, P], F32, name="share_t")
         for t in range(PACK):
             nc.tensor.matmul(
                 share_t[:], share[:, t, :], ident[:],
                 start=(t == 0), stop=(t == PACK - 1), is_transpose=True,
             )
+        weight = sb.tile([P, PACK, M], F32, name="weight")
+        for t in range(PACK):
+            nc.scalar.activation(weight[:, t, :], share[:, t, :], ACT.Copy, scale=fac_sb[:, t : t + 1])
+        nc.scalar.copy(
+            rows_w2[:, :I].rearrange("p (m t) -> p m t", t=PACK),
+            weight[:].rearrange("p t m -> p m t"),
+        )
         share_sb = sb.tile([P, P], F32, name="share_sb")
         col_sum = sb.tile([P, 1], F32, name="col_sum")
         nc.scalar.activation(share_sb[:], share_t[:], ACT.Copy, accum_out=col_sum[:])
 
         turned2 = gather_and_turn(2)
-        rows_w0 = sb.tile([P, 2 * I], BF16, name="rows_w0", tag="big2", align_bytes=64)
-        weave(turned0, rows_w0[:, I:])
-        weave(turned2, rows12[:, I:])
-        nc.vector.tensor_tensor(
-            rows_w0[:, :I].rearrange("p (m t) -> p m t", t=PACK),
-            share[:].rearrange("p t m -> p m t"),
-            fac_sb[:].unsqueeze(1).to_broadcast([P, M, PACK]),
-            ALU.mult,
-        )
-        rows3 = sb.tile([P, I], BF16, name="rows3", tag="rows3", align_bytes=64)
+        v01 = quantise("v01", rows01[:], behind(2, 0, [P, 2 * P], U32, "v01_codes"))
+        weave(turned2, rows_w2[:, I:])
         weave(gather_and_turn(3), rows3[:])
-        w0_mx = quantise("w0", rows_w0[:], 2 * P, "big3")
-        v12 = quantise("v12", rows12[:], 2 * P, "big2")
-        col_inv = sb.tile([P, 1], F32, name="col_inv", tag="rows12", align_bytes=64)
+        w2 = quantise("w2", rows_w2[:], behind(3, 0, [P, 2 * P], U32, "w2_codes"))
+        col_inv = behind(3, 1024, [P, 1], F32, "col_inv")
         nc.vector.reciprocal(col_inv[:], col_sum[:])
-        v3 = quantise("v3", rows3[:], P, "v3_codes")
+        v3_codes = sb.tile([P, P], U32, name="v3_codes", align_bytes=64)
+        v3 = quantise("v3", rows3[:], v3_codes)
         z012 = ps.tile([P, 3 * P], F32, name="z012")
         z3 = ps.tile([P, P], F32, name="z3")
-        multiply(z012[:, :P], w0_mx, M)
-        multiply(z012[:, P:], v12, 0)
-        multiply(z3[:], v3, 0)
+        multiply(z012[:, : 2 * P], w2, v01, 0)
+        multiply(z012[:, 2 * P :], w2, w2, M)
+        multiply(z3[:], w2, v3, 0)
         mean012 = sb.tile([P, 3 * P], F32, name="mean012")
         nc.scalar.activation(mean012[:], z012[:], ACT.Copy, scale=col_inv[:])
         nc.sync.dma_start(out[:, : 3 * P], mean012[:])
         mean3 = sb.tile([P, P], F32, name="mean3")
-        nc.vector.tensor_scalar(mean3[:], z3[:], col_inv[:], None, ALU.mult)
-        nc.sync.dma_start(out[:, 3 * P :], mean3[:])
+        nc.scalar.activation(mean3[:], z3[:], ACT.Copy, scale=col_inv[:])
+        nc.scalar.dma_start(out[:, 3 * P :], mean3[:])

@@ -21,6 +21,7 @@ P = 128
 PACK = 4
 BLOCKS = E // P
 ROW = 4 * T
+HALF = P // 2
 
 
 def tile_attend_clustermeans_kernel(tc, pts_words, pts_scales, cent, fac, vals, offs, out):
@@ -34,8 +35,6 @@ def tile_attend_clustermeans_kernel(tc, pts_words, pts_scales, cent, fac, vals, 
         word_pool = sb.tile([P, T], U16, name="word_pool", align_bytes=64)
         nc.sync.dma_start(word_pool[:].bitcast(I32), pts_words[0].bitcast(I32))
         nc.sync.dma_start(offsets[:], offs)
-        cent_raw = sb.tile([P, PACK, M], F32, name="cent_raw")
-        nc.sync.dma_start(cent_raw[:], cent.rearrange("(p t) m -> p t m", t=PACK))
 
         byte_pool = sb.tile([P, T], U8, name="byte_pool", align_bytes=64)
         nc.vector.memset(byte_pool[:].bitcast(I32), 0)
@@ -44,27 +43,29 @@ def tile_attend_clustermeans_kernel(tc, pts_words, pts_scales, cent, fac, vals, 
                 byte_pool[32 * q : 32 * q + 4, :].bitcast(I32),
                 pts_scales[0, 4 * q : 4 * q + 4, :].bitcast(I32),
             )
-        zeros = big.tile([P, BLOCKS * T], F32, name="zeros", offset=0, align_bytes=64)
+        zeros = big.tile([P, BLOCKS * T + I + PACK], F32, name="zeros", offset=0, align_bytes=64)
         nc.gpsimd.memset(zeros[:, :P], 0.0)
         ident = sb.tile([P, P], F32, name="ident")
         nc.gpsimd.affine_select(
             out=ident[:], in_=zeros[:, :P], compare_op=ALU.not_equal, fill=1.0,
             base=0, pattern=[[-1, P]], channel_multiplier=1,
         )
+        cent_raw = big.tile([P, PACK, M], F32, name="cent_raw", offset=BLOCKS * ROW, align_bytes=64)
+        nc.sync.dma_start(cent_raw[:], cent.rearrange("(p t) m -> p t m", t=PACK))
         val_pool = []
         for b in range(BLOCKS):
             tile_b = big.tile([P, T], F32, name="val_pool%d" % b, offset=b * ROW, align_bytes=64)
             nc.sync.dma_start(tile_b[:], vals[b * P : (b + 1) * P, :])
             val_pool.append(tile_b)
-        fac_sb = sb.tile([P, PACK], F32, name="fac_sb")
+        fac_sb = big.tile([P, PACK], F32, name="fac_sb", offset=BLOCKS * ROW + 4 * I, align_bytes=64)
         nc.gpsimd.dma_start(fac_sb[:], fac.rearrange("(p t) o -> p (t o)", t=PACK))
 
         word_list = sb.tile([P, I], U16, name="word_list", align_bytes=64)
         nc.vector.tensor_copy(word_list[:], word_pool[:].indirect(offsets[:]))
-        word_dealt = sb.tile([P, PACK, P], U16, name="word_dealt", align_bytes=64)
-        nc.vector.tensor_copy(word_dealt[:], word_list[:].rearrange("p (s t) -> p t s", t=PACK))
         byte_list = sb.tile([P, I], U8, name="byte_list", align_bytes=64)
         nc.vector.tensor_copy(byte_list[:], byte_pool[:].indirect(offsets[:]))
+        word_dealt = sb.tile([P, PACK, P], U16, name="word_dealt", align_bytes=64)
+        nc.vector.tensor_copy(word_dealt[:], word_list[:].rearrange("p (s t) -> p t s", t=PACK))
         byte_dealt = sb.tile([P, PACK, P], U8, name="byte_dealt", align_bytes=64)
         nc.vector.tensor_copy(byte_dealt[:], byte_list[:].rearrange("p (s t) -> p t s", t=PACK))
 
@@ -81,7 +82,7 @@ def tile_attend_clustermeans_kernel(tc, pts_words, pts_scales, cent, fac, vals, 
         cent_codes = sb.tile([P, M], U32, name="cent_codes", align_bytes=64)
         cent_mx = quantise("cent", cent_bf[:].rearrange("p m t -> p (m t)"), cent_codes)
 
-        scores = ps.tile([P, PACK, M], F32, name="scores")
+        scores = ps.tile([P, PACK, M], F32, name="scores", tag="scores")
         for t in range(PACK):
             nc.tensor.matmul_mx(
                 out=scores[:, t, :],
@@ -124,7 +125,6 @@ def tile_attend_clustermeans_kernel(tc, pts_words, pts_scales, cent, fac, vals, 
 
         rows01 = sb.tile([P, 2 * I], BF16, name="rows01", align_bytes=64)
         rows_w2 = sb.tile([P, 2 * I], BF16, name="rows_w2", align_bytes=64)
-        rows3 = sb.tile([P, I], BF16, name="rows3", align_bytes=64)
 
         turned0 = gather_and_turn(0)
         neg_max = behind(0, 0, [P, PACK], F32, "neg_max")
@@ -144,7 +144,7 @@ def tile_attend_clustermeans_kernel(tc, pts_words, pts_scales, cent, fac, vals, 
         for t in range(PACK):
             nc.scalar.activation(share[:, t, :], expd[:, t, :], ACT.Copy, scale=row_inv[:, t : t + 1])
         weave(turned1, rows01[:, I:])
-        share_t = ps.tile([P, P], F32, name="share_t")
+        share_t = ps.tile([P, P], F32, name="share_t", tag="scores")
         for t in range(PACK):
             nc.tensor.matmul(
                 share_t[:], share[:, t, :], ident[:],
@@ -164,20 +164,35 @@ def tile_attend_clustermeans_kernel(tc, pts_words, pts_scales, cent, fac, vals, 
         turned2 = gather_and_turn(2)
         v01 = quantise("v01", rows01[:], behind(2, 0, [P, 2 * P], U32, "v01_codes"))
         weave(turned2, rows_w2[:, I:])
-        weave(gather_and_turn(3), rows3[:])
+        turned3 = gather_and_turn(3)
+        halves = []
+        for h in range(2):
+            rows_h = sb.tile([P, I // 2], BF16, name="rows3_%d" % h, align_bytes=64)
+            nc.scalar.copy(
+                rows_h[:].bitcast(F32).rearrange("p (e u) -> p e u", u=2),
+                turned3[:, :, h * HALF : (h + 1) * HALF].rearrange("p u e -> p e u"),
+            )
+            halves.append(rows_h)
         w2 = quantise("w2", rows_w2[:], behind(3, 0, [P, 2 * P], U32, "w2_codes"))
         col_inv = behind(3, 1024, [P, 1], F32, "col_inv")
         nc.vector.reciprocal(col_inv[:], col_sum[:])
-        v3_codes = sb.tile([P, P], U32, name="v3_codes", align_bytes=64)
-        v3 = quantise("v3", rows3[:], v3_codes)
-        z012 = ps.tile([P, 3 * P], F32, name="z012")
-        z3 = ps.tile([P, P], F32, name="z3")
-        multiply(z012[:, : 2 * P], w2, v01, 0)
-        multiply(z012[:, 2 * P :], w2, w2, M)
-        multiply(z3[:], w2, v3, 0)
-        mean012 = sb.tile([P, 3 * P], F32, name="mean012")
-        nc.scalar.activation(mean012[:], z012[:], ACT.Copy, scale=col_inv[:])
-        nc.sync.dma_start(out[:, : 3 * P], mean012[:])
+        v3 = []
+        for h in range(2):
+            codes_h = sb.tile([P, HALF], U32, name="v3_codes%d" % h, align_bytes=64)
+            v3.append(quantise("v3_%d" % h, halves[h][:], codes_h))
+        z01 = ps.tile([P, 2 * P], F32, name="z01")
+        multiply(z01[:], w2, v01, 0)
+        mean01 = sb.tile([P, 2 * P], F32, name="mean01")
+        nc.scalar.activation(mean01[:], z01[:], ACT.Copy, scale=col_inv[:])
+        nc.sync.dma_start(out[:, : 2 * P], mean01[:])
+        z2 = ps.tile([P, P], F32, name="z2")
+        multiply(z2[:], w2, w2, M)
+        mean2 = sb.tile([P, P], F32, name="mean2")
+        nc.scalar.activation(mean2[:], z2[:], ACT.Copy, scale=col_inv[:])
+        nc.sync.dma_start(out[:, 2 * P : 3 * P], mean2[:])
         mean3 = sb.tile([P, P], F32, name="mean3")
-        nc.scalar.activation(mean3[:], z3[:], ACT.Copy, scale=col_inv[:])
+        for h in range(2):
+            z_h = ps.tile([P, HALF], F32, name="z3_%d" % h)
+            multiply(z_h[:], w2, v3[h], 0)
+            nc.scalar.activation(mean3[:, h * HALF : (h + 1) * HALF], z_h[:], ACT.Copy, scale=col_inv[:])
         nc.scalar.dma_start(out[:, 3 * P :], mean3[:])

@@ -38,10 +38,10 @@ def tile_attend_clustermeans_kernel(tc, pts_words, pts_scales, cent, fac, vals, 
 
         byte_pool = sb.tile([P, T], U8, name="byte_pool", align_bytes=64)
         nc.vector.memset(byte_pool[:].bitcast(I32), 0)
-        for q in range(4):
+        for r in range(4):
             nc.sync.dma_start(
-                byte_pool[32 * q : 32 * q + 4, :].bitcast(I32),
-                pts_scales[0, 4 * q : 4 * q + 4, :].bitcast(I32),
+                byte_pool[r:P:32, :].bitcast(I32),
+                pts_scales[0, r:16:4, :].bitcast(I32),
             )
         zeros = big.tile([P, BLOCKS * T + I + PACK], F32, name="zeros", offset=0, align_bytes=64)
         nc.gpsimd.memset(zeros[:, :P], 0.0)

@@ -35,6 +35,8 @@ def tile_attend_clustermeans_kernel(tc, pts_words, pts_scales, cent, fac, vals, 
         word_pool = sb.tile([P, T], U16, name="word_pool", align_bytes=64)
         nc.sync.dma_start(word_pool[:].bitcast(I32), pts_words[0].bitcast(I32))
         nc.sync.dma_start(offsets[:], offs)
+        cent_raw = sb.tile([P, PACK, M], F32, name="cent_raw")
+        nc.sync.dma_start(cent_raw[:], cent.rearrange("(p t) m -> p t m", t=PACK))
 
         byte_pool = sb.tile([P, T], U8, name="byte_pool", align_bytes=64)
         nc.vector.memset(byte_pool[:].bitcast(I32), 0)
@@ -43,22 +45,21 @@ def tile_attend_clustermeans_kernel(tc, pts_words, pts_scales, cent, fac, vals, 
                 byte_pool[r:P:32, :].bitcast(I32),
                 pts_scales[0, r:16:4, :].bitcast(I32),
             )
-        zeros = big.tile([P, BLOCKS * T + I + PACK], F32, name="zeros", offset=0, align_bytes=64)
+        zeros = big.tile([P, BLOCKS * T + PACK], F32, name="zeros", offset=0, align_bytes=64)
         nc.gpsimd.memset(zeros[:, :P], 0.0)
         ident = sb.tile([P, P], F32, name="ident")
         nc.gpsimd.affine_select(
             out=ident[:], in_=zeros[:, :P], compare_op=ALU.not_equal, fill=1.0,
             base=0, pattern=[[-1, P]], channel_multiplier=1,
         )
-        cent_raw = big.tile([P, PACK, M], F32, name="cent_raw", offset=BLOCKS * ROW, align_bytes=64)
-        nc.sync.dma_start(cent_raw[:], cent.rearrange("(p t) m -> p t m", t=PACK))
         val_pool = []
         for b in range(BLOCKS):
             tile_b = big.tile([P, T], F32, name="val_pool%d" % b, offset=b * ROW, align_bytes=64)
             nc.sync.dma_start(tile_b[:], vals[b * P : (b + 1) * P, :])
             val_pool.append(tile_b)
-        fac_sb = big.tile([P, PACK], F32, name="fac_sb", offset=BLOCKS * ROW + 4 * I, align_bytes=64)
-        nc.gpsimd.dma_start(fac_sb[:], fac.rearrange("(p t) o -> p (t o)", t=PACK))
+            if b == 0:
+                fac_sb = big.tile([P, PACK], F32, name="fac_sb", offset=BLOCKS * ROW, align_bytes=64)
+                nc.sync.dma_start(fac_sb[:], fac.rearrange("(p t) o -> p (t o)", t=PACK))
 
         word_list = sb.tile([P, I], U16, name="word_list", align_bytes=64)
         nc.vector.tensor_copy(word_list[:], word_pool[:].indirect(offsets[:]))
@@ -124,7 +125,6 @@ def tile_attend_clustermeans_kernel(tc, pts_words, pts_scales, cent, fac, vals, 
             )
 
         rows01 = sb.tile([P, 2 * I], BF16, name="rows01", align_bytes=64)
-        rows_w2 = sb.tile([P, 2 * I], BF16, name="rows_w2", align_bytes=64)
 
         turned0 = gather_and_turn(0)
         neg_max = behind(0, 0, [P, PACK], F32, "neg_max")
@@ -140,29 +140,30 @@ def tile_attend_clustermeans_kernel(tc, pts_words, pts_scales, cent, fac, vals, 
         turned1 = gather_and_turn(1)
         row_inv = behind(1, 0, [P, PACK], F32, "row_inv")
         nc.vector.reciprocal(row_inv[:], row_sum[:])
+        factor = sb.tile([P, PACK], F32, name="factor")
+        nc.vector.tensor_tensor(factor[:], row_inv[:], fac_sb[:], ALU.mult)
+        weight = sb.tile([P, PACK, M], F32, name="weight")
+        for t in range(PACK):
+            nc.scalar.activation(weight[:, t, :], expd[:, t, :], ACT.Copy, scale=factor[:, t : t + 1])
+        weave(turned1, rows01[:, I:])
         share = sb.tile([P, PACK, M], F32, name="share")
         for t in range(PACK):
             nc.scalar.activation(share[:, t, :], expd[:, t, :], ACT.Copy, scale=row_inv[:, t : t + 1])
-        weave(turned1, rows01[:, I:])
         share_t = ps.tile([P, P], F32, name="share_t", tag="scores")
         for t in range(PACK):
             nc.tensor.matmul(
                 share_t[:], share[:, t, :], ident[:],
                 start=(t == 0), stop=(t == PACK - 1), is_transpose=True,
             )
-        weight = sb.tile([P, PACK, M], F32, name="weight")
-        for t in range(PACK):
-            nc.scalar.activation(weight[:, t, :], share[:, t, :], ACT.Copy, scale=fac_sb[:, t : t + 1])
-        nc.scalar.copy(
-            rows_w2[:, :I].rearrange("p (m t) -> p m t", t=PACK),
-            weight[:].rearrange("p t m -> p m t"),
-        )
         share_sb = sb.tile([P, P], F32, name="share_sb")
         col_sum = sb.tile([P, 1], F32, name="col_sum")
         nc.scalar.activation(share_sb[:], share_t[:], ACT.Copy, accum_out=col_sum[:])
 
         turned2 = gather_and_turn(2)
-        v01 = quantise("v01", rows01[:], behind(2, 0, [P, 2 * P], U32, "v01_codes"))
+        rows_w2 = behind(2, 0, [P, 2 * I], BF16, "rows_w2")
+        nc.vector.tensor_copy(
+            rows_w2[:, :I].rearrange("p (m t) -> p m t", t=PACK), weight[:].rearrange("p t m -> p m t")
+        )
         weave(turned2, rows_w2[:, I:])
         turned3 = gather_and_turn(3)
         halves = []
@@ -174,6 +175,7 @@ def tile_attend_clustermeans_kernel(tc, pts_words, pts_scales, cent, fac, vals, 
             )
             halves.append(rows_h)
         w2 = quantise("w2", rows_w2[:], behind(3, 0, [P, 2 * P], U32, "w2_codes"))
+        v01 = quantise("v01", rows01[:], behind(3, 2048, [P, 2 * P], U32, "v01_codes"))
         col_inv = behind(3, 1024, [P, 1], F32, "col_inv")
         nc.vector.reciprocal(col_inv[:], col_sum[:])
         v3 = []

@@ -98,7 +98,7 @@ def tile_attend_clustermeans_kernel(tc, pts_words, pts_scales, cent, fac, vals, 
         seen = []
 
         def gather_and_turn(b):
-            listed = sb.tile([P, I], BF16, name="listed%d" % b, align_bytes=64)
+            listed = sb.tile([P, I], BF16, name="listed%d" % b, tag="listed%d" % b, align_bytes=64)
             nc.vector.tensor_copy(listed[:], val_pool[b][:].indirect(offsets[:]))
             seen.append(listed)
             pairs = listed[:].bitcast(F32)
@@ -141,7 +141,8 @@ def tile_attend_clustermeans_kernel(tc, pts_words, pts_scales, cent, fac, vals, 
         row_inv = behind(1, 0, [P, PACK], F32, "row_inv")
         nc.vector.reciprocal(row_inv[:], row_sum[:])
         factor = sb.tile([P, PACK], F32, name="factor")
-        nc.vector.tensor_tensor(factor[:], row_inv[:], fac_sb[:], ALU.mult)
+        for t in range(PACK):
+            nc.scalar.activation(factor[:, t : t + 1], fac_sb[:, t : t + 1], ACT.Copy, scale=row_inv[:, t : t + 1])
         weight = sb.tile([P, PACK, M], F32, name="weight")
         for t in range(PACK):
             nc.scalar.activation(weight[:, t, :], expd[:, t, :], ACT.Copy, scale=factor[:, t : t + 1])
@@ -155,9 +156,6 @@ def tile_attend_clustermeans_kernel(tc, pts_words, pts_scales, cent, fac, vals, 
                 share_t[:], share[:, t, :], ident[:],
                 start=(t == 0), stop=(t == PACK - 1), is_transpose=True,
             )
-        share_sb = sb.tile([P, P], F32, name="share_sb")
-        col_sum = sb.tile([P, 1], F32, name="col_sum")
-        nc.scalar.activation(share_sb[:], share_t[:], ACT.Copy, accum_out=col_sum[:])
 
         turned2 = gather_and_turn(2)
         rows_w2 = behind(2, 0, [P, 2 * I], BF16, "rows_w2")
@@ -165,6 +163,9 @@ def tile_attend_clustermeans_kernel(tc, pts_words, pts_scales, cent, fac, vals, 
             rows_w2[:, :I].rearrange("p (m t) -> p m t", t=PACK), weight[:].rearrange("p t m -> p m t")
         )
         weave(turned2, rows_w2[:, I:])
+        share_sb = sb.tile([P, P], F32, name="share_sb", tag="listed2", align_bytes=64)
+        col_sum = sb.tile([P, 1], F32, name="col_sum")
+        nc.scalar.activation(share_sb[:], share_t[:], ACT.Copy, accum_out=col_sum[:])
         turned3 = gather_and_turn(3)
         halves = []
         for h in range(2):

@@ -1,6 +1,7 @@
 from contextlib import ExitStack
 
 import concourse.mybir as mybir
+from concourse.masks import make_identity
 
 D, T, I, M, E = 512, 2048, 512, 128, 512
 FLOPS = 2 * I * D * M + 2 * M * I * E
@@ -29,14 +30,15 @@ def tile_attend_clustermeans_kernel(tc, pts_words, pts_scales, cent, fac, vals, 
     with ExitStack() as ctx:
         sb = ctx.enter_context(tc.tile_pool(name="sb", bufs=1))
         big = ctx.enter_context(tc.tile_pool(name="big", bufs=1))
+        head = ctx.enter_context(tc.tile_pool(name="head", bufs=1))
         ps = ctx.enter_context(tc.psum_pool(name="ps", bufs=1))
 
         offsets = sb.tile([P, I // 16], U16, name="offsets")
+        nc.sync.dma_start(offsets[:], offs)
         word_pool = sb.tile([P, T], U16, name="word_pool", align_bytes=64)
         nc.sync.dma_start(word_pool[:].bitcast(I32), pts_words[0].bitcast(I32))
-        nc.sync.dma_start(offsets[:], offs)
-        cent_raw = sb.tile([P, PACK, M], F32, name="cent_raw")
-        nc.sync.dma_start(cent_raw[:], cent.rearrange("(p t) m -> p t m", t=PACK))
+        fac_sb = sb.tile([P, PACK], F32, name="fac_sb", align_bytes=64)
+        nc.sync.dma_start(fac_sb[:], fac.rearrange("(p t) o -> p (t o)", t=PACK))
 
         byte_pool = sb.tile([P, T], U8, name="byte_pool", align_bytes=64)
         nc.vector.memset(byte_pool[:].bitcast(I32), 0)
@@ -45,30 +47,20 @@ def tile_attend_clustermeans_kernel(tc, pts_words, pts_scales, cent, fac, vals, 
                 byte_pool[r:P:32, :].bitcast(I32),
                 pts_scales[0, r:16:4, :].bitcast(I32),
             )
-        zeros = big.tile([P, BLOCKS * T + PACK], F32, name="zeros", offset=0, align_bytes=64)
-        nc.gpsimd.memset(zeros[:, :P], 0.0)
+        cent_raw = head.tile([P, PACK, M], F32, name="cent_raw", offset=0, align_bytes=64)
+        nc.sync.dma_start(cent_raw[:], cent.rearrange("(p t) m -> p t m", t=PACK))
         ident = sb.tile([P, P], F32, name="ident")
-        nc.gpsimd.affine_select(
-            out=ident[:], in_=zeros[:, :P], compare_op=ALU.not_equal, fill=1.0,
-            base=0, pattern=[[-1, P]], channel_multiplier=1,
-        )
+        make_identity(nc, ident[:])
         val_pool = []
         for b in range(BLOCKS):
             tile_b = big.tile([P, T], F32, name="val_pool%d" % b, offset=b * ROW, align_bytes=64)
             nc.sync.dma_start(tile_b[:], vals[b * P : (b + 1) * P, :])
             val_pool.append(tile_b)
-            if b == 0:
-                fac_sb = big.tile([P, PACK], F32, name="fac_sb", offset=BLOCKS * ROW, align_bytes=64)
-                nc.sync.dma_start(fac_sb[:], fac.rearrange("(p t) o -> p (t o)", t=PACK))
 
         word_list = sb.tile([P, I], U16, name="word_list", align_bytes=64)
         nc.vector.tensor_copy(word_list[:], word_pool[:].indirect(offsets[:]))
         byte_list = sb.tile([P, I], U8, name="byte_list", align_bytes=64)
         nc.vector.tensor_copy(byte_list[:], byte_pool[:].indirect(offsets[:]))
-        word_dealt = sb.tile([P, PACK, P], U16, name="word_dealt", align_bytes=64)
-        nc.vector.tensor_copy(word_dealt[:], word_list[:].rearrange("p (s t) -> p t s", t=PACK))
-        byte_dealt = sb.tile([P, PACK, P], U8, name="byte_dealt", align_bytes=64)
-        nc.vector.tensor_copy(byte_dealt[:], byte_list[:].rearrange("p (s t) -> p t s", t=PACK))
 
         def quantise(name, rows, codes):
             plane = sb.tile([P, codes.shape[1]], U8, name=name + "_bytes", align_bytes=64)
@@ -83,6 +75,11 @@ def tile_attend_clustermeans_kernel(tc, pts_words, pts_scales, cent, fac, vals, 
         cent_codes = sb.tile([P, M], U32, name="cent_codes", align_bytes=64)
         cent_mx = quantise("cent", cent_bf[:].rearrange("p m t -> p (m t)"), cent_codes)
 
+        word_dealt = head.tile([P, PACK, P], U16, name="word_dealt", offset=0, align_bytes=64)
+        nc.vector.tensor_copy(word_dealt[:], word_list[:].rearrange("p (s t) -> p t s", t=PACK))
+        byte_dealt = head.tile([P, PACK, P], U8, name="byte_dealt", offset=1024, align_bytes=64)
+        nc.vector.tensor_copy(byte_dealt[:], byte_list[:].rearrange("p (s t) -> p t s", t=PACK))
+
         scores = ps.tile([P, PACK, M], F32, name="scores", tag="scores")
         for t in range(PACK):
             nc.tensor.matmul_mx(
@@ -95,12 +92,9 @@ def tile_attend_clustermeans_kernel(tc, pts_words, pts_scales, cent, fac, vals, 
                 stop=True,
             )
 
-        seen = []
-
         def gather_and_turn(b):
             listed = sb.tile([P, I], BF16, name="listed%d" % b, tag="listed%d" % b, align_bytes=64)
             nc.vector.tensor_copy(listed[:], val_pool[b][:].indirect(offsets[:]))
-            seen.append(listed)
             pairs = listed[:].bitcast(F32)
             turned = ps.tile([P, 2, P], F32, name="turned%d" % b, tag="turned%d" % (b % 3))
             for u in range(2):

@@ -34,11 +34,9 @@ def tile_attend_clustermeans_kernel(tc, pts_words, pts_scales, cent, fac, vals, 
         ps = ctx.enter_context(tc.psum_pool(name="ps", bufs=1))
 
         offsets = sb.tile([P, I // 16], U16, name="offsets")
-        nc.sync.dma_start(offsets[:], offs)
         word_pool = sb.tile([P, T], U16, name="word_pool", align_bytes=64)
         nc.sync.dma_start(word_pool[:].bitcast(I32), pts_words[0].bitcast(I32))
-        fac_sb = sb.tile([P, PACK], F32, name="fac_sb", align_bytes=64)
-        nc.sync.dma_start(fac_sb[:], fac.rearrange("(p t) o -> p (t o)", t=PACK))
+        nc.sync.dma_start(offsets[:], offs)
 
         byte_pool = sb.tile([P, T], U8, name="byte_pool", align_bytes=64)
         nc.vector.memset(byte_pool[:].bitcast(I32), 0)
@@ -56,6 +54,9 @@ def tile_attend_clustermeans_kernel(tc, pts_words, pts_scales, cent, fac, vals, 
             tile_b = big.tile([P, T], F32, name="val_pool%d" % b, offset=b * ROW, align_bytes=64)
             nc.sync.dma_start(tile_b[:], vals[b * P : (b + 1) * P, :])
             val_pool.append(tile_b)
+            if b == 0:
+                fac_sb = sb.tile([P, PACK], F32, name="fac_sb", align_bytes=64)
+                nc.sync.dma_start(fac_sb[:], fac.rearrange("(p t) o -> p (t o)", t=PACK))
 
         word_list = sb.tile([P, I], U16, name="word_list", align_bytes=64)
         nc.vector.tensor_copy(word_list[:], word_pool[:].indirect(offsets[:]))
@@ -71,7 +72,10 @@ def tile_attend_clustermeans_kernel(tc, pts_words, pts_scales, cent, fac, vals, 
             return big.tile(shape, dtype, name=name, offset=b * ROW + at, align_bytes=64)
 
         cent_bf = sb.tile([P, M, PACK], BF16, name="cent_bf", align_bytes=64)
-        nc.scalar.copy(cent_bf[:], cent_raw[:].rearrange("p t m -> p m t"))
+        nc.scalar.copy(
+            cent_bf[:].rearrange("p (c i) t -> p c t i", i=PACK),
+            cent_raw[:].rearrange("p t (c i) -> p c t i", i=PACK),
+        )
         cent_codes = sb.tile([P, M], U32, name="cent_codes", align_bytes=64)
         cent_mx = quantise("cent", cent_bf[:].rearrange("p m t -> p (m t)"), cent_codes)
 
@@ -94,11 +98,13 @@ def tile_attend_clustermeans_kernel(tc, pts_words, pts_scales, cent, fac, vals, 
 
         def gather_and_turn(b):
             listed = sb.tile([P, I], BF16, name="listed%d" % b, tag="listed%d" % b, align_bytes=64)
-            nc.vector.tensor_copy(listed[:], val_pool[b][:].indirect(offsets[:]))
+            nc.vector.tensor_copy(
+                listed[:].rearrange("p (u s v) -> p s u v", u=2, v=2), val_pool[b][:].indirect(offsets[:])
+            )
             pairs = listed[:].bitcast(F32)
             turned = ps.tile([P, 2, P], F32, name="turned%d" % b, tag="turned%d" % (b % 3))
             for u in range(2):
-                nc.tensor.transpose(turned[:, u, :], pairs[:, u : 2 * P : 2], ident[:])
+                nc.tensor.transpose(turned[:, u, :], pairs[:, u * P : (u + 1) * P], ident[:])
             return turned
 
         def weave(turned, rows):
@@ -107,13 +113,13 @@ def tile_attend_clustermeans_kernel(tc, pts_words, pts_scales, cent, fac, vals, 
                 turned[:].rearrange("p u e -> p e u"),
             )
 
-        def multiply(z, weights, moving, first):
+        def multiply(z, weights, moving):
             nc.tensor.matmul_mx(
                 out=z,
-                lhsT=weights[0][:, :M].bitcast(FP8X4),
-                lhsT_scale=weights[1][:, :M],
-                rhs=moving[0][:, first:].bitcast(FP8X4),
-                rhs_scale=moving[1][:, first:],
+                lhsT=weights[0][:].bitcast(FP8X4),
+                lhsT_scale=weights[1][:],
+                rhs=moving[0][:].bitcast(FP8X4),
+                rhs_scale=moving[1][:],
                 start=True,
                 stop=True,
             )
@@ -121,6 +127,7 @@ def tile_attend_clustermeans_kernel(tc, pts_words, pts_scales, cent, fac, vals, 
         rows01 = sb.tile([P, 2 * I], BF16, name="rows01", align_bytes=64)
 
         turned0 = gather_and_turn(0)
+        weave(turned0, rows01[:, :I])
         neg_max = behind(0, 0, [P, PACK], F32, "neg_max")
         nc.vector.tensor_reduce(neg_max[:], scores[:], axis=AXIS.X, op=ALU.max, negate=True)
         expd = sb.tile([P, PACK, M], F32, name="expd")
@@ -130,17 +137,21 @@ def tile_attend_clustermeans_kernel(tc, pts_words, pts_scales, cent, fac, vals, 
                 expd[:, t, :], scores[:, t, :], ACT.Exp,
                 bias=neg_max[:, t : t + 1], accum_out=row_sum[:, t : t + 1],
             )
-        weave(turned0, rows01[:, :I])
-        turned1 = gather_and_turn(1)
-        row_inv = behind(1, 0, [P, PACK], F32, "row_inv")
-        nc.vector.reciprocal(row_inv[:], row_sum[:])
-        factor = sb.tile([P, PACK], F32, name="factor")
+        scaled = sb.tile([P, PACK, M], F32, name="scaled")
         for t in range(PACK):
-            nc.scalar.activation(factor[:, t : t + 1], fac_sb[:, t : t + 1], ACT.Copy, scale=row_inv[:, t : t + 1])
+            nc.scalar.activation(scaled[:, t, :], expd[:, t, :], ACT.Copy, scale=fac_sb[:, t : t + 1])
+        turned1 = gather_and_turn(1)
+        row_inv = sb.tile([P, PACK], F32, name="row_inv")
+        nc.vector.reciprocal(row_inv[:], row_sum[:])
         weight = sb.tile([P, PACK, M], F32, name="weight")
         for t in range(PACK):
-            nc.scalar.activation(weight[:, t, :], expd[:, t, :], ACT.Copy, scale=factor[:, t : t + 1])
+            nc.scalar.activation(weight[:, t, :], scaled[:, t, :], ACT.Copy, scale=row_inv[:, t : t + 1])
         weave(turned1, rows01[:, I:])
+        rows_w = sb.tile([P, I], BF16, name="rows_w", align_bytes=64)
+        nc.scalar.copy(
+            rows_w[:].rearrange("p (c i t) -> p c t i", i=PACK, t=PACK),
+            weight[:].rearrange("p t (c i) -> p c t i", i=PACK),
+        )
         share = sb.tile([P, PACK, M], F32, name="share")
         for t in range(PACK):
             nc.scalar.activation(share[:, t, :], expd[:, t, :], ACT.Copy, scale=row_inv[:, t : t + 1])
@@ -152,15 +163,22 @@ def tile_attend_clustermeans_kernel(tc, pts_words, pts_scales, cent, fac, vals, 
             )
 
         turned2 = gather_and_turn(2)
-        rows_w2 = behind(2, 0, [P, 2 * I], BF16, "rows_w2")
-        nc.vector.tensor_copy(
-            rows_w2[:, :I].rearrange("p (m t) -> p m t", t=PACK), weight[:].rearrange("p t m -> p m t")
-        )
-        weave(turned2, rows_w2[:, I:])
+        v01 = quantise("v01", rows01[:], behind(2, 0, [P, 2 * P], U32, "v01_codes"))
+        w_mx = quantise("w", rows_w[:], behind(2, 2048, [P, P], U32, "w_codes"))
+        rows2 = sb.tile([P, I], BF16, name="rows2", align_bytes=64)
+        weave(turned2, rows2[:])
         share_sb = sb.tile([P, P], F32, name="share_sb", tag="listed2", align_bytes=64)
         col_sum = sb.tile([P, 1], F32, name="col_sum")
         nc.scalar.activation(share_sb[:], share_t[:], ACT.Copy, accum_out=col_sum[:])
+        z01 = ps.tile([P, 2 * P], F32, name="z01")
+        multiply(z01[:], w_mx, v01)
         turned3 = gather_and_turn(3)
+        col_inv = behind(3, 1024, [P, 1], F32, "col_inv")
+        nc.vector.reciprocal(col_inv[:], col_sum[:])
+        v2 = quantise("v2", rows2[:], behind(3, 0, [P, P], U32, "v2_codes"))
+        mean01 = sb.tile([P, 2 * P], F32, name="mean01")
+        nc.vector.tensor_scalar_mul(mean01[:], z01[:], col_inv[:])
+        nc.sync.dma_start(out[:, : 2 * P], mean01[:])
         halves = []
         for h in range(2):
             rows_h = sb.tile([P, I // 2], BF16, name="rows3_%d" % h, align_bytes=64)
@@ -169,27 +187,18 @@ def tile_attend_clustermeans_kernel(tc, pts_words, pts_scales, cent, fac, vals, 
                 turned3[:, :, h * HALF : (h + 1) * HALF].rearrange("p u e -> p e u"),
             )
             halves.append(rows_h)
-        w2 = quantise("w2", rows_w2[:], behind(3, 0, [P, 2 * P], U32, "w2_codes"))
-        v01 = quantise("v01", rows01[:], behind(3, 2048, [P, 2 * P], U32, "v01_codes"))
-        col_inv = behind(3, 1024, [P, 1], F32, "col_inv")
-        nc.vector.reciprocal(col_inv[:], col_sum[:])
         v3 = []
         for h in range(2):
             codes_h = sb.tile([P, HALF], U32, name="v3_codes%d" % h, align_bytes=64)
             v3.append(quantise("v3_%d" % h, halves[h][:], codes_h))
-        z01 = ps.tile([P, 2 * P], F32, name="z01")
-        multiply(z01[:], w2, v01, 0)
-        mean01 = sb.tile([P, 2 * P], F32, name="mean01")
-        nc.scalar.activation(mean01[:], z01[:], ACT.Copy, scale=col_inv[:])
-        nc.sync.dma_start(out[:, : 2 * P], mean01[:])
         z2 = ps.tile([P, P], F32, name="z2")
-        multiply(z2[:], w2, w2, M)
+        multiply(z2[:], w_mx, v2)
         mean2 = sb.tile([P, P], F32, name="mean2")
         nc.scalar.activation(mean2[:], z2[:], ACT.Copy, scale=col_inv[:])
         nc.sync.dma_start(out[:, 2 * P : 3 * P], mean2[:])
         mean3 = sb.tile([P, P], F32, name="mean3")
         for h in range(2):
             z_h = ps.tile([P, HALF], F32, name="z3_%d" % h)
-            multiply(z_h[:], w2, v3[h], 0)
+            multiply(z_h[:], w_mx, v3[h])
             nc.scalar.activation(mean3[:, h * HALF : (h + 1) * HALF], z_h[:], ACT.Copy, scale=col_inv[:])
         nc.scalar.dma_start(out[:, 3 * P :], mean3[:])

@@ -23,6 +23,7 @@ PACK = 4
 BLOCKS = E // P
 ROW = 4 * T
 HALF = P // 2
+RUN = 8
 
 
 def tile_attend_clustermeans_kernel(tc, pts_words, pts_scales, cent, fac, vals, offs, out):
@@ -47,6 +48,8 @@ def tile_attend_clustermeans_kernel(tc, pts_words, pts_scales, cent, fac, vals, 
             )
         cent_raw = head.tile([P, PACK, M], F32, name="cent_raw", offset=0, align_bytes=64)
         nc.sync.dma_start(cent_raw[:], cent.rearrange("(p t) m -> p t m", t=PACK))
+        fac_rows = sb.tile([P, P], F32, name="fac_rows")
+        nc.gpsimd.memset(fac_rows[:], 0.0)
         ident = sb.tile([P, P], F32, name="ident")
         make_identity(nc, ident[:])
         val_pool = []
@@ -55,8 +58,10 @@ def tile_attend_clustermeans_kernel(tc, pts_words, pts_scales, cent, fac, vals, 
             nc.sync.dma_start(tile_b[:], vals[b * P : (b + 1) * P, :])
             val_pool.append(tile_b)
             if b == 0:
-                fac_sb = sb.tile([P, PACK], F32, name="fac_sb", align_bytes=64)
-                nc.sync.dma_start(fac_sb[:], fac.rearrange("(p t) o -> p (t o)", t=PACK))
+                nc.sync.dma_start(
+                    fac_rows[:PACK, :].rearrange("t (j q) -> t j q", q=RUN),
+                    fac.rearrange("(j t q) o -> t j (q o)", t=PACK, q=RUN),
+                )
 
         word_list = sb.tile([P, I], U16, name="word_list", align_bytes=64)
         nc.vector.tensor_copy(word_list[:], word_pool[:].indirect(offsets[:]))
@@ -80,9 +85,15 @@ def tile_attend_clustermeans_kernel(tc, pts_words, pts_scales, cent, fac, vals, 
         cent_mx = quantise("cent", cent_bf[:].rearrange("p m t -> p (m t)"), cent_codes)
 
         word_dealt = head.tile([P, PACK, P], U16, name="word_dealt", offset=0, align_bytes=64)
-        nc.vector.tensor_copy(word_dealt[:], word_list[:].rearrange("p (s t) -> p t s", t=PACK))
+        nc.vector.tensor_copy(
+            word_dealt[:].bitcast(I32).rearrange("p t (j q) -> p t j q", q=RUN // 2),
+            word_list[:].bitcast(I32).rearrange("p (j t q) -> p t j q", t=PACK, q=RUN // 2),
+        )
         byte_dealt = head.tile([P, PACK, P], U8, name="byte_dealt", offset=1024, align_bytes=64)
-        nc.vector.tensor_copy(byte_dealt[:], byte_list[:].rearrange("p (s t) -> p t s", t=PACK))
+        nc.vector.tensor_copy(
+            byte_dealt[:].bitcast(I32).rearrange("p t (j q) -> p t j q", q=RUN // 4),
+            byte_list[:].bitcast(I32).rearrange("p (j t q) -> p t j q", t=PACK, q=RUN // 4),
+        )
 
         scores = ps.tile([P, PACK, M], F32, name="scores", tag="scores")
         for t in range(PACK):
@@ -96,10 +107,16 @@ def tile_attend_clustermeans_kernel(tc, pts_words, pts_scales, cent, fac, vals, 
                 stop=True,
             )
 
+        fac_t = ps.tile([P, P], F32, name="fac_t", tag="z3_1")
+        nc.tensor.transpose(fac_t[:], fac_rows[:], ident[:])
+        fac_sb = sb.tile([P, PACK], F32, name="fac_sb")
+        nc.scalar.copy(fac_sb[:], fac_t[:, :PACK])
+
         def gather_and_turn(b):
             listed = sb.tile([P, I], BF16, name="listed%d" % b, tag="listed%d" % b, align_bytes=64)
             nc.vector.tensor_copy(
-                listed[:].rearrange("p (u s v) -> p s u v", u=2, v=2), val_pool[b][:].indirect(offsets[:])
+                listed[:].rearrange("p (u j q v) -> p j u v q", u=2, q=RUN, v=2),
+                val_pool[b][:].indirect(offsets[:]),
             )
             pairs = listed[:].bitcast(F32)
             turned = ps.tile([P, 2, P], F32, name="turned%d" % b, tag="turned%d" % (b % 3))
@@ -141,7 +158,7 @@ def tile_attend_clustermeans_kernel(tc, pts_words, pts_scales, cent, fac, vals, 
         for t in range(PACK):
             nc.scalar.activation(scaled[:, t, :], expd[:, t, :], ACT.Copy, scale=fac_sb[:, t : t + 1])
         turned1 = gather_and_turn(1)
-        row_inv = sb.tile([P, PACK], F32, name="row_inv")
+        row_inv = behind(1, 0, [P, PACK], F32, "row_inv")
         nc.vector.reciprocal(row_inv[:], row_sum[:])
         weight = sb.tile([P, PACK, M], F32, name="weight")
         for t in range(PACK):
@@ -198,7 +215,7 @@ def tile_attend_clustermeans_kernel(tc, pts_words, pts_scales, cent, fac, vals, 
         nc.sync.dma_start(out[:, 2 * P : 3 * P], mean2[:])
         mean3 = sb.tile([P, P], F32, name="mean3")
         for h in range(2):
-            z_h = ps.tile([P, HALF], F32, name="z3_%d" % h)
+            z_h = ps.tile([P, HALF], F32, name="z3_%d" % h, tag="z3_%d" % h)
             multiply(z_h[:], w_mx, v3[h])
             nc.scalar.activation(mean3[:, h * HALF : (h + 1) * HALF], z_h[:], ACT.Copy, scale=col_inv[:])
         nc.scalar.dma_start(out[:, 3 * P :], mean3[:])

@@ -48,7 +48,7 @@ def tile_attend_clustermeans_kernel(tc, pts_words, pts_scales, cent, fac, vals, 
             )
         cent_raw = head.tile([P, PACK, M], F32, name="cent_raw", offset=0, align_bytes=64)
         nc.sync.dma_start(cent_raw[:], cent.rearrange("(p t) m -> p t m", t=PACK))
-        fac_rows = sb.tile([P, P], F32, name="fac_rows")
+        fac_rows = sb.tile([P, I], F32, name="fac_rows")
         nc.gpsimd.memset(fac_rows[:], 0.0)
         ident = sb.tile([P, P], F32, name="ident")
         make_identity(nc, ident[:])
@@ -58,10 +58,8 @@ def tile_attend_clustermeans_kernel(tc, pts_words, pts_scales, cent, fac, vals, 
             nc.sync.dma_start(tile_b[:], vals[b * P : (b + 1) * P, :])
             val_pool.append(tile_b)
             if b == 0:
-                nc.sync.dma_start(
-                    fac_rows[:PACK, :].rearrange("t (j q) -> t j q", q=RUN),
-                    fac.rearrange("(j t q) o -> t j (q o)", t=PACK, q=RUN),
-                )
+                fac_line = sb.tile([1, I], F32, name="fac_line")
+                nc.sync.dma_start(fac_line[:], fac.rearrange("i o -> o i"))
 
         word_list = sb.tile([P, I], U16, name="word_list", align_bytes=64)
         nc.vector.tensor_copy(word_list[:], word_pool[:].indirect(offsets[:]))
@@ -107,10 +105,15 @@ def tile_attend_clustermeans_kernel(tc, pts_words, pts_scales, cent, fac, vals, 
                 stop=True,
             )
 
-        fac_t = ps.tile([P, P], F32, name="fac_t", tag="z3_1")
-        nc.tensor.transpose(fac_t[:], fac_rows[:], ident[:])
+        nc.scalar.copy(
+            fac_rows[0:1, :].rearrange("o (t j q) -> o t j q", t=PACK, q=RUN),
+            fac_line[:].rearrange("o (j t q) -> o t j q", t=PACK, q=RUN),
+        )
+        fac_t = ps.tile([P, PACK, P], F32, name="fac_t", tag="z3_1")
+        for t in range(PACK):
+            nc.tensor.transpose(fac_t[:, t, :], fac_rows[:, t * P : (t + 1) * P], ident[:])
         fac_sb = sb.tile([P, PACK], F32, name="fac_sb")
-        nc.scalar.copy(fac_sb[:], fac_t[:, :PACK])
+        nc.scalar.copy(fac_sb[:], fac_t[:, :, 0])
 
         def gather_and_turn(b):
             listed = sb.tile([P, I], BF16, name="listed%d" % b, tag="listed%d" % b, align_bytes=64)
@@ -218,4 +221,4 @@ def tile_attend_clustermeans_kernel(tc, pts_words, pts_scales, cent, fac, vals, 
             z_h = ps.tile([P, HALF], F32, name="z3_%d" % h, tag="z3_%d" % h)
             multiply(z_h[:], w_mx, v3[h])
             nc.scalar.activation(mean3[:, h * HALF : (h + 1) * HALF], z_h[:], ACT.Copy, scale=col_inv[:])
-        nc.scalar.dma_start(out[:, 3 * P :], mean3[:])
+        nc.sync.dma_start(out[:, 3 * P :], mean3[:])

@@ -24,6 +24,7 @@ BLOCKS = E // P
 ROW = 4 * T
 HALF = P // 2
 RUN = 8
+SPLITS = (320, 256, 512, 320)
 
 
 def tile_attend_clustermeans_kernel(tc, pts_words, pts_scales, cent, fac, vals, offs, out):
@@ -40,7 +41,7 @@ def tile_attend_clustermeans_kernel(tc, pts_words, pts_scales, cent, fac, vals, 
         nc.sync.dma_start(offsets[:], offs)
 
         byte_pool = sb.tile([P, T], U8, name="byte_pool", align_bytes=64)
-        nc.vector.memset(byte_pool[:].bitcast(I32), 0)
+        nc.gpsimd.memset(byte_pool[:].bitcast(I32), 0)
         for r in range(4):
             nc.sync.dma_start(
                 byte_pool[r:P:32, :].bitcast(I32),
@@ -58,13 +59,12 @@ def tile_attend_clustermeans_kernel(tc, pts_words, pts_scales, cent, fac, vals, 
             nc.sync.dma_start(tile_b[:], vals[b * P : (b + 1) * P, :])
             val_pool.append(tile_b)
             if b == 0:
-                fac_line = sb.tile([1, I], F32, name="fac_line")
-                nc.sync.dma_start(fac_line[:], fac.rearrange("i o -> o i"))
+                nc.sync.dma_start(fac_rows[0:1, :], fac.rearrange("i o -> o i"))
 
         word_list = sb.tile([P, I], U16, name="word_list", align_bytes=64)
         nc.vector.tensor_copy(word_list[:], word_pool[:].indirect(offsets[:]))
-        byte_list = sb.tile([P, I], U8, name="byte_list", align_bytes=64)
-        nc.vector.tensor_copy(byte_list[:], byte_pool[:].indirect(offsets[:]))
+        byte_dealt = sb.tile([P, PACK, P], U8, name="byte_dealt", align_bytes=64)
+        nc.vector.tensor_copy(byte_dealt[:].rearrange("p t s -> p s t"), byte_pool[:].indirect(offsets[:]))
 
         def quantise(name, rows, codes):
             plane = sb.tile([P, codes.shape[1]], U8, name=name + "_bytes", align_bytes=64)
@@ -84,13 +84,8 @@ def tile_attend_clustermeans_kernel(tc, pts_words, pts_scales, cent, fac, vals, 
 
         word_dealt = head.tile([P, PACK, P], U16, name="word_dealt", offset=0, align_bytes=64)
         nc.vector.tensor_copy(
-            word_dealt[:].bitcast(I32).rearrange("p t (j q) -> p t j q", q=RUN // 2),
-            word_list[:].bitcast(I32).rearrange("p (j t q) -> p t j q", t=PACK, q=RUN // 2),
-        )
-        byte_dealt = head.tile([P, PACK, P], U8, name="byte_dealt", offset=1024, align_bytes=64)
-        nc.vector.tensor_copy(
-            byte_dealt[:].bitcast(I32).rearrange("p t (j q) -> p t j q", q=RUN // 4),
-            byte_list[:].bitcast(I32).rearrange("p (j t q) -> p t j q", t=PACK, q=RUN // 4),
+            word_dealt[:].rearrange("p t (c i) -> p c t i", i=RUN),
+            word_list[:].rearrange("p (c i t) -> p c t i", t=PACK, i=RUN),
         )
 
         scores = ps.tile([P, PACK, M], F32, name="scores", tag="scores")
@@ -105,26 +100,22 @@ def tile_attend_clustermeans_kernel(tc, pts_words, pts_scales, cent, fac, vals, 
                 stop=True,
             )
 
-        nc.scalar.copy(
-            fac_rows[0:1, :].rearrange("o (t j q) -> o t j q", t=PACK, q=RUN),
-            fac_line[:].rearrange("o (j t q) -> o t j q", t=PACK, q=RUN),
-        )
         fac_t = ps.tile([P, PACK, P], F32, name="fac_t", tag="z3_1")
         for t in range(PACK):
-            nc.tensor.transpose(fac_t[:, t, :], fac_rows[:, t * P : (t + 1) * P], ident[:])
+            nc.tensor.transpose(fac_t[:, t, :], fac_rows[:, t:I:PACK], ident[:])
         fac_sb = sb.tile([P, PACK], F32, name="fac_sb")
         nc.scalar.copy(fac_sb[:], fac_t[:, :, 0])
 
         def gather_and_turn(b):
             listed = sb.tile([P, I], BF16, name="listed%d" % b, tag="listed%d" % b, align_bytes=64)
-            nc.vector.tensor_copy(
-                listed[:].rearrange("p (u j q v) -> p j u v q", u=2, q=RUN, v=2),
-                val_pool[b][:].indirect(offsets[:]),
-            )
+            split = SPLITS[b]
+            nc.vector.tensor_copy(listed[:, :split], val_pool[b][:].indirect(offsets[:, : split // 16]))
+            if split < I:
+                nc.scalar.activation(listed[:, split:], val_pool[b][:].indirect(offsets[:, split // 16 :]), ACT.Copy)
             pairs = listed[:].bitcast(F32)
             turned = ps.tile([P, 2, P], F32, name="turned%d" % b, tag="turned%d" % (b % 3))
             for u in range(2):
-                nc.tensor.transpose(turned[:, u, :], pairs[:, u * P : (u + 1) * P], ident[:])
+                nc.tensor.transpose(turned[:, u, :], pairs[:, u : 2 * P : 2], ident[:])
             return turned
 
         def weave(turned, rows):
@@ -147,7 +138,6 @@ def tile_attend_clustermeans_kernel(tc, pts_words, pts_scales, cent, fac, vals, 
         rows01 = sb.tile([P, 2 * I], BF16, name="rows01", align_bytes=64)
 
         turned0 = gather_and_turn(0)
-        weave(turned0, rows01[:, :I])
         neg_max = behind(0, 0, [P, PACK], F32, "neg_max")
         nc.vector.tensor_reduce(neg_max[:], scores[:], axis=AXIS.X, op=ALU.max, negate=True)
         expd = sb.tile([P, PACK, M], F32, name="expd")
@@ -157,24 +147,23 @@ def tile_attend_clustermeans_kernel(tc, pts_words, pts_scales, cent, fac, vals, 
                 expd[:, t, :], scores[:, t, :], ACT.Exp,
                 bias=neg_max[:, t : t + 1], accum_out=row_sum[:, t : t + 1],
             )
-        scaled = sb.tile([P, PACK, M], F32, name="scaled")
-        for t in range(PACK):
-            nc.scalar.activation(scaled[:, t, :], expd[:, t, :], ACT.Copy, scale=fac_sb[:, t : t + 1])
         turned1 = gather_and_turn(1)
-        row_inv = behind(1, 0, [P, PACK], F32, "row_inv")
+        weave(turned0, rows01[:, :I])
+        row_inv = sb.tile([P, PACK], F32, name="row_inv")
         nc.vector.reciprocal(row_inv[:], row_sum[:])
-        weight = sb.tile([P, PACK, M], F32, name="weight")
-        for t in range(PACK):
-            nc.scalar.activation(weight[:, t, :], scaled[:, t, :], ACT.Copy, scale=row_inv[:, t : t + 1])
-        weave(turned1, rows01[:, I:])
+        factor = sb.tile([P, PACK], F32, name="factor")
+        nc.vector.tensor_tensor(factor[:], row_inv[:], fac_sb[:], ALU.mult)
         rows_w = sb.tile([P, I], BF16, name="rows_w", align_bytes=64)
-        nc.scalar.copy(
+        nc.vector.tensor_tensor(
             rows_w[:].rearrange("p (c i t) -> p c t i", i=PACK, t=PACK),
-            weight[:].rearrange("p t (c i) -> p c t i", i=PACK),
+            expd[:].rearrange("p t (c i) -> p c t i", i=PACK),
+            factor[:].unsqueeze(1).unsqueeze(3).to_broadcast([P, M // PACK, PACK, PACK]),
+            ALU.mult,
         )
         share = sb.tile([P, PACK, M], F32, name="share")
         for t in range(PACK):
             nc.scalar.activation(share[:, t, :], expd[:, t, :], ACT.Copy, scale=row_inv[:, t : t + 1])
+        weave(turned1, rows01[:, I:])
         share_t = ps.tile([P, P], F32, name="share_t", tag="scores")
         for t in range(PACK):
             nc.tensor.matmul(
@@ -182,23 +171,23 @@ def tile_attend_clustermeans_kernel(tc, pts_words, pts_scales, cent, fac, vals, 
                 start=(t == 0), stop=(t == PACK - 1), is_transpose=True,
             )
 
+        share_sb = sb.tile([P, P], F32, name="share_sb")
+        col_sum = sb.tile([P, 1], F32, name="col_sum")
+        nc.scalar.activation(share_sb[:], share_t[:], ACT.Copy, accum_out=col_sum[:])
         turned2 = gather_and_turn(2)
         v01 = quantise("v01", rows01[:], behind(2, 0, [P, 2 * P], U32, "v01_codes"))
         w_mx = quantise("w", rows_w[:], behind(2, 2048, [P, P], U32, "w_codes"))
-        rows2 = sb.tile([P, I], BF16, name="rows2", align_bytes=64)
-        weave(turned2, rows2[:])
-        share_sb = sb.tile([P, P], F32, name="share_sb", tag="listed2", align_bytes=64)
-        col_sum = sb.tile([P, 1], F32, name="col_sum")
-        nc.scalar.activation(share_sb[:], share_t[:], ACT.Copy, accum_out=col_sum[:])
+        col_inv = behind(2, 4096, [P, 1], F32, "col_inv")
+        nc.vector.reciprocal(col_inv[:], col_sum[:])
         z01 = ps.tile([P, 2 * P], F32, name="z01")
         multiply(z01[:], w_mx, v01)
         turned3 = gather_and_turn(3)
-        col_inv = behind(3, 1024, [P, 1], F32, "col_inv")
-        nc.vector.reciprocal(col_inv[:], col_sum[:])
-        v2 = quantise("v2", rows2[:], behind(3, 0, [P, P], U32, "v2_codes"))
-        mean01 = sb.tile([P, 2 * P], F32, name="mean01")
+        rows2 = behind(3, 4096, [P, I], BF16, "rows2")
+        weave(turned2, rows2[:])
+        mean01 = behind(3, 1024, [P, 2 * P], F32, "mean01")
         nc.vector.tensor_scalar_mul(mean01[:], z01[:], col_inv[:])
         nc.sync.dma_start(out[:, : 2 * P], mean01[:])
+        v2 = quantise("v2", rows2[:], sb.tile([P, P], U32, name="v2_codes", align_bytes=64))
         halves = []
         for h in range(2):
             rows_h = sb.tile([P, I // 2], BF16, name="rows3_%d" % h, align_bytes=64)

@@ -41,7 +41,7 @@ def tile_attend_clustermeans_kernel(tc, pts_words, pts_scales, cent, fac, vals, 
         nc.sync.dma_start(offsets[:], offs)
 
         byte_pool = sb.tile([P, T], U8, name="byte_pool", align_bytes=64)
-        nc.gpsimd.memset(byte_pool[:].bitcast(I32), 0)
+        nc.vector.memset(byte_pool[:].bitcast(I32), 0)
         for r in range(4):
             nc.sync.dma_start(
                 byte_pool[r:P:32, :].bitcast(I32),
@@ -50,7 +50,7 @@ def tile_attend_clustermeans_kernel(tc, pts_words, pts_scales, cent, fac, vals, 
         cent_raw = head.tile([P, PACK, M], F32, name="cent_raw", offset=0, align_bytes=64)
         nc.sync.dma_start(cent_raw[:], cent.rearrange("(p t) m -> p t m", t=PACK))
         fac_rows = sb.tile([P, I], F32, name="fac_rows")
-        nc.gpsimd.memset(fac_rows[:], 0.0)
+        nc.vector.memset(fac_rows[:], 0.0)
         ident = sb.tile([P, P], F32, name="ident")
         make_identity(nc, ident[:])
         val_pool = []
@@ -118,8 +118,8 @@ def tile_attend_clustermeans_kernel(tc, pts_words, pts_scales, cent, fac, vals, 
                 nc.tensor.transpose(turned[:, u, :], pairs[:, u : 2 * P : 2], ident[:])
             return turned
 
-        def weave(turned, rows):
-            nc.scalar.copy(
+        def weave(turned, rows, copy=nc.scalar.copy):
+            copy(
                 rows.bitcast(F32).rearrange("p (e u) -> p e u", u=2),
                 turned[:].rearrange("p u e -> p e u"),
             )
@@ -183,7 +183,7 @@ def tile_attend_clustermeans_kernel(tc, pts_words, pts_scales, cent, fac, vals, 
         multiply(z01[:], w_mx, v01)
         turned3 = gather_and_turn(3)
         rows2 = behind(3, 4096, [P, I], BF16, "rows2")
-        weave(turned2, rows2[:])
+        weave(turned2, rows2[:], nc.vector.tensor_copy)
         mean01 = behind(3, 1024, [P, 2 * P], F32, "mean01")
         nc.vector.tensor_scalar_mul(mean01[:], z01[:], col_inv[:])
         nc.sync.dma_start(out[:, : 2 * P], mean01[:])
@@ -203,7 +203,7 @@ def tile_attend_clustermeans_kernel(tc, pts_words, pts_scales, cent, fac, vals, 
         z2 = ps.tile([P, P], F32, name="z2")
         multiply(z2[:], w_mx, v2)
         mean2 = sb.tile([P, P], F32, name="mean2")
-        nc.scalar.activation(mean2[:], z2[:], ACT.Copy, scale=col_inv[:])
+        nc.vector.tensor_scalar_mul(mean2[:], z2[:], col_inv[:])
         nc.sync.dma_start(out[:, 2 * P : 3 * P], mean2[:])
         mean3 = sb.tile([P, P], F32, name="mean3")
         for h in range(2):

@@ -24,7 +24,7 @@ BLOCKS = E // P
 ROW = 4 * T
 HALF = P // 2
 RUN = 8
-SPLITS = (320, 256, 512, 320)
+SPLITS = (320, 512, 0, 320)
 
 
 def tile_attend_clustermeans_kernel(tc, pts_words, pts_scales, cent, fac, vals, offs, out):
@@ -109,7 +109,8 @@ def tile_attend_clustermeans_kernel(tc, pts_words, pts_scales, cent, fac, vals, 
         def gather_and_turn(b):
             listed = sb.tile([P, I], BF16, name="listed%d" % b, tag="listed%d" % b, align_bytes=64)
             split = SPLITS[b]
-            nc.vector.tensor_copy(listed[:, :split], val_pool[b][:].indirect(offsets[:, : split // 16]))
+            if split > 0:
+                nc.vector.tensor_copy(listed[:, :split], val_pool[b][:].indirect(offsets[:, : split // 16]))
             if split < I:
                 nc.scalar.activation(listed[:, split:], val_pool[b][:].indirect(offsets[:, split // 16 :]), ACT.Copy)
             pairs = listed[:].bitcast(F32)
@@ -149,10 +150,12 @@ def tile_attend_clustermeans_kernel(tc, pts_words, pts_scales, cent, fac, vals, 
             )
         turned1 = gather_and_turn(1)
         weave(turned0, rows01[:, :I])
-        row_inv = sb.tile([P, PACK], F32, name="row_inv")
+        row_inv = behind(1, 0, [P, PACK], F32, "row_inv")
         nc.vector.reciprocal(row_inv[:], row_sum[:])
         factor = sb.tile([P, PACK], F32, name="factor")
         nc.vector.tensor_tensor(factor[:], row_inv[:], fac_sb[:], ALU.mult)
+        share = sb.tile([P, PACK, M], F32, name="share")
+        nc.vector.tensor_tensor(share[:], expd[:], row_inv[:].unsqueeze(2).to_broadcast([P, PACK, M]), ALU.mult)
         rows_w = sb.tile([P, I], BF16, name="rows_w", align_bytes=64)
         nc.vector.tensor_tensor(
             rows_w[:].rearrange("p (c i t) -> p c t i", i=PACK, t=PACK),
@@ -160,28 +163,25 @@ def tile_attend_clustermeans_kernel(tc, pts_words, pts_scales, cent, fac, vals, 
             factor[:].unsqueeze(1).unsqueeze(3).to_broadcast([P, M // PACK, PACK, PACK]),
             ALU.mult,
         )
-        share = sb.tile([P, PACK, M], F32, name="share")
-        for t in range(PACK):
-            nc.scalar.activation(share[:, t, :], expd[:, t, :], ACT.Copy, scale=row_inv[:, t : t + 1])
         weave(turned1, rows01[:, I:])
-        share_t = ps.tile([P, P], F32, name="share_t", tag="scores")
+        share_t = ps.tile([P, P], F32, name="share_t", tag="turned1")
         for t in range(PACK):
             nc.tensor.matmul(
                 share_t[:], share[:, t, :], ident[:],
                 start=(t == 0), stop=(t == PACK - 1), is_transpose=True,
             )
 
-        share_sb = sb.tile([P, P], F32, name="share_sb")
+        v01 = quantise("v01", rows01[:], sb.tile([P, 2 * P], U32, name="v01_codes", align_bytes=64))
+        w_mx = quantise("w", rows_w[:], sb.tile([P, P], U32, name="w_codes", align_bytes=64))
+        turned2 = gather_and_turn(2)
+        share_sb = behind(2, 0, [P, P], F32, "share_sb")
         col_sum = sb.tile([P, 1], F32, name="col_sum")
         nc.scalar.activation(share_sb[:], share_t[:], ACT.Copy, accum_out=col_sum[:])
-        turned2 = gather_and_turn(2)
-        v01 = quantise("v01", rows01[:], behind(2, 0, [P, 2 * P], U32, "v01_codes"))
-        w_mx = quantise("w", rows_w[:], behind(2, 2048, [P, P], U32, "w_codes"))
-        col_inv = behind(2, 4096, [P, 1], F32, "col_inv")
-        nc.vector.reciprocal(col_inv[:], col_sum[:])
         z01 = ps.tile([P, 2 * P], F32, name="z01")
         multiply(z01[:], w_mx, v01)
         turned3 = gather_and_turn(3)
+        col_inv = behind(3, 0, [P, 1], F32, "col_inv")
+        nc.vector.reciprocal(col_inv[:], col_sum[:])
         rows2 = behind(3, 4096, [P, I], BF16, "rows2")
         weave(turned2, rows2[:], nc.vector.tensor_copy)
         mean01 = behind(3, 1024, [P, 2 * P], F32, "mean01")

@@ -24,7 +24,7 @@ BLOCKS = E // P
 ROW = 4 * T
 HALF = P // 2
 RUN = 8
-SPLITS = (320, 512, 0, 320)
+SPLITS = (320, 384, 0, 288)
 
 
 def tile_attend_clustermeans_kernel(tc, pts_words, pts_scales, cent, fac, vals, offs, out):
@@ -88,10 +88,10 @@ def tile_attend_clustermeans_kernel(tc, pts_words, pts_scales, cent, fac, vals, 
             word_list[:].rearrange("p (c i t) -> p c t i", t=PACK, i=RUN),
         )
 
-        scores = ps.tile([P, PACK, M], F32, name="scores", tag="scores")
+        scores = [ps.tile([P, 2, M], F32, name="scores%d" % g, tag="scores%d" % g) for g in range(2)]
         for t in range(PACK):
             nc.tensor.matmul_mx(
-                out=scores[:, t, :],
+                out=scores[t // 2][:, t % 2, :],
                 lhsT=word_dealt[:, t, :].bitcast(FP4X4),
                 lhsT_scale=byte_dealt[:, t, :],
                 rhs=cent_mx[0][:].bitcast(FP8X4),
@@ -119,8 +119,8 @@ def tile_attend_clustermeans_kernel(tc, pts_words, pts_scales, cent, fac, vals, 
                 nc.tensor.transpose(turned[:, u, :], pairs[:, u : 2 * P : 2], ident[:])
             return turned
 
-        def weave(turned, rows, copy=nc.scalar.copy):
-            copy(
+        def weave(turned, rows):
+            nc.scalar.copy(
                 rows.bitcast(F32).rearrange("p (e u) -> p e u", u=2),
                 turned[:].rearrange("p u e -> p e u"),
             )
@@ -140,12 +140,13 @@ def tile_attend_clustermeans_kernel(tc, pts_words, pts_scales, cent, fac, vals, 
 
         turned0 = gather_and_turn(0)
         neg_max = behind(0, 0, [P, PACK], F32, "neg_max")
-        nc.vector.tensor_reduce(neg_max[:], scores[:], axis=AXIS.X, op=ALU.max, negate=True)
+        for g in range(2):
+            nc.vector.tensor_reduce(neg_max[:, 2 * g : 2 * g + 2], scores[g][:], axis=AXIS.X, op=ALU.max, negate=True)
         expd = sb.tile([P, PACK, M], F32, name="expd")
         row_sum = sb.tile([P, PACK], F32, name="row_sum")
         for t in range(PACK):
             nc.scalar.activation(
-                expd[:, t, :], scores[:, t, :], ACT.Exp,
+                expd[:, t, :], scores[t // 2][:, t % 2, :], ACT.Exp,
                 bias=neg_max[:, t : t + 1], accum_out=row_sum[:, t : t + 1],
             )
         turned1 = gather_and_turn(1)
@@ -174,16 +175,15 @@ def tile_attend_clustermeans_kernel(tc, pts_words, pts_scales, cent, fac, vals, 
         v01 = quantise("v01", rows01[:], sb.tile([P, 2 * P], U32, name="v01_codes", align_bytes=64))
         w_mx = quantise("w", rows_w[:], sb.tile([P, P], U32, name="w_codes", align_bytes=64))
         turned2 = gather_and_turn(2)
-        share_sb = behind(2, 0, [P, P], F32, "share_sb")
         col_sum = sb.tile([P, 1], F32, name="col_sum")
-        nc.scalar.activation(share_sb[:], share_t[:], ACT.Copy, accum_out=col_sum[:])
+        nc.vector.tensor_reduce(col_sum[:], share_t[:], axis=AXIS.X, op=ALU.add)
+        col_inv = sb.tile([P, 1], F32, name="col_inv")
+        nc.vector.reciprocal(col_inv[:], col_sum[:])
         z01 = ps.tile([P, 2 * P], F32, name="z01")
         multiply(z01[:], w_mx, v01)
         turned3 = gather_and_turn(3)
-        col_inv = behind(3, 0, [P, 1], F32, "col_inv")
-        nc.vector.reciprocal(col_inv[:], col_sum[:])
         rows2 = behind(3, 4096, [P, I], BF16, "rows2")
-        weave(turned2, rows2[:], nc.vector.tensor_copy)
+        weave(turned2, rows2[:])
         mean01 = behind(3, 1024, [P, 2 * P], F32, "mean01")
         nc.vector.tensor_scalar_mul(mean01[:], z01[:], col_inv[:])
         nc.sync.dma_start(out[:, : 2 * P], mean01[:])
@@ -200,7 +200,7 @@ def tile_attend_clustermeans_kernel(tc, pts_words, pts_scales, cent, fac, vals, 
         for h in range(2):
             codes_h = sb.tile([P, HALF], U32, name="v3_codes%d" % h, align_bytes=64)
             v3.append(quantise("v3_%d" % h, halves[h][:], codes_h))
-        z2 = ps.tile([P, P], F32, name="z2")
+        z2 = ps.tile([P, P], F32, name="z2", tag="scores1")
         multiply(z2[:], w_mx, v2)
         mean2 = sb.tile([P, P], F32, name="mean2")
         nc.vector.tensor_scalar_mul(mean2[:], z2[:], col_inv[:])

@@ -24,6 +24,9 @@ BLOCKS = E // P
 ROW = 4 * T
 HALF = P // 2
 RUN = 8
+SCALE_ROWS = D // 32
+SCALE_AT = 16
+FAC_AT = 4
 SPLITS = (320, 384, 0, 288)
 
 
@@ -32,114 +35,121 @@ def tile_attend_clustermeans_kernel(tc, pts_words, pts_scales, cent, fac, vals, 
     with ExitStack() as ctx:
         sb = ctx.enter_context(tc.tile_pool(name="sb", bufs=1))
         big = ctx.enter_context(tc.tile_pool(name="big", bufs=1))
-        head = ctx.enter_context(tc.tile_pool(name="head", bufs=1))
         ps = ctx.enter_context(tc.psum_pool(name="ps", bufs=1))
 
         offsets = sb.tile([P, I // 16], U16, name="offsets")
-        word_pool = sb.tile([P, T], U16, name="word_pool", align_bytes=64)
-        nc.sync.dma_start(word_pool[:].bitcast(I32), pts_words[0].bitcast(I32))
         nc.sync.dma_start(offsets[:], offs)
-
-        byte_pool = sb.tile([P, T], U8, name="byte_pool", align_bytes=64)
-        nc.vector.memset(byte_pool[:].bitcast(I32), 0)
-        for r in range(4):
-            nc.sync.dma_start(
-                byte_pool[r:P:32, :].bitcast(I32),
-                pts_scales[0, r:16:4, :].bitcast(I32),
-            )
-        cent_raw = head.tile([P, PACK, M], F32, name="cent_raw", offset=0, align_bytes=64)
+        byte_pool = big.tile([P, T], U8, name="byte_pool", offset=2 * ROW - T // 2, align_bytes=64)
+        nc.scalar.dma_start(byte_pool[SCALE_AT : SCALE_AT + SCALE_ROWS, :].bitcast(I32), pts_scales[0].bitcast(I32))
+        for lo, hi in ((0, SCALE_AT), (32, 64), (64, P)):
+            nc.vector.memset(byte_pool[lo:hi, :].bitcast(I32), 0)
+        word_pool = big.tile([P, T], U16, name="word_pool", offset=3 * ROW, align_bytes=64)
+        nc.sync.dma_start(word_pool[:].bitcast(I32), pts_words[0].bitcast(I32))
+        cent_raw = sb.tile([P, PACK, M], F32, name="cent_raw", align_bytes=64)
         nc.sync.dma_start(cent_raw[:], cent.rearrange("(p t) m -> p t m", t=PACK))
         fac_rows = sb.tile([P, I], F32, name="fac_rows")
         nc.vector.memset(fac_rows[:], 0.0)
+        nc.sync.dma_start(fac_rows[FAC_AT : FAC_AT + 1, :], fac.rearrange("i o -> o i"))
+        key_plane = sb.tile([P, PACK, P], U8, name="key_plane", align_bytes=64)
+        plane_words = key_plane[:].rearrange("p t s -> p (t s)").bitcast(I32)
+        nc.vector.memset(plane_words, 0)
         ident = sb.tile([P, P], F32, name="ident")
         make_identity(nc, ident[:])
+
         val_pool = []
-        for b in range(BLOCKS):
+
+        def load_block(b):
             tile_b = big.tile([P, T], F32, name="val_pool%d" % b, offset=b * ROW, align_bytes=64)
             nc.sync.dma_start(tile_b[:], vals[b * P : (b + 1) * P, :])
             val_pool.append(tile_b)
-            if b == 0:
-                nc.sync.dma_start(fac_rows[0:1, :], fac.rearrange("i o -> o i"))
 
-        word_list = sb.tile([P, I], U16, name="word_list", align_bytes=64)
-        nc.vector.tensor_copy(word_list[:], word_pool[:].indirect(offsets[:]))
+        load_block(0)
+
         byte_dealt = sb.tile([P, PACK, P], U8, name="byte_dealt", align_bytes=64)
         nc.vector.tensor_copy(byte_dealt[:].rearrange("p t s -> p s t"), byte_pool[:].indirect(offsets[:]))
+        dealt_words = byte_dealt[:].rearrange("p t s -> p (t s)").bitcast(I32)
+        for r in range(4):
+            nc.sync.dma_start(plane_words[r:P:32, :], dealt_words[SCALE_AT + r : SCALE_AT + SCALE_ROWS : 4, :])
+        word_list = sb.tile([P, I], U16, name="word_list", align_bytes=64)
+        nc.vector.tensor_copy(word_list[:], word_pool[:].indirect(offsets[:]))
+        for b in range(1, BLOCKS):
+            load_block(b)
 
-        def quantise(name, rows, codes):
-            plane = sb.tile([P, codes.shape[1]], U8, name=name + "_bytes", align_bytes=64)
-            nc.vector.quantize_mx(out=codes[:].bitcast(FP8X4), scales=plane[:], in_=rows)
+        def quantise(name, rows, codes, plane):
+            nc.vector.quantize_mx(out=codes.bitcast(FP8X4), scales=plane, in_=rows)
             return codes, plane
 
-        def behind(b, at, shape, dtype, name):
-            return big.tile(shape, dtype, name=name, offset=b * ROW + at, align_bytes=64)
+        def mx_tiles(name, width):
+            codes = sb.tile([P, width], U32, name=name + "_codes", align_bytes=64)
+            plane = sb.tile([P, width], U8, name=name + "_bytes", align_bytes=64)
+            return codes, plane
 
         cent_bf = sb.tile([P, M, PACK], BF16, name="cent_bf", align_bytes=64)
         nc.scalar.copy(
             cent_bf[:].rearrange("p (c i) t -> p c t i", i=PACK),
             cent_raw[:].rearrange("p t (c i) -> p c t i", i=PACK),
         )
-        cent_codes = sb.tile([P, M], U32, name="cent_codes", align_bytes=64)
-        cent_mx = quantise("cent", cent_bf[:].rearrange("p m t -> p (m t)"), cent_codes)
-
-        word_dealt = head.tile([P, PACK, P], U16, name="word_dealt", offset=0, align_bytes=64)
+        word_dealt = sb.tile([P, PACK, P], U16, name="word_dealt", align_bytes=64)
         nc.vector.tensor_copy(
             word_dealt[:].rearrange("p t (c i) -> p c t i", i=RUN),
             word_list[:].rearrange("p (c i t) -> p c t i", t=PACK, i=RUN),
         )
+        cent_codes, cent_plane = mx_tiles("cent", M)
+        quantise("cent", cent_bf[:].rearrange("p m t -> p (m t)"), cent_codes[:], cent_plane[:])
+
+        fac_t = ps.tile([P, PACK, P], F32, name="fac_t", tag="turn_a")
+        for t in range(PACK):
+            nc.tensor.transpose(fac_t[:, t, :], fac_rows[:, t:I:PACK], ident[:])
+        fac_sb = sb.tile([P, PACK], F32, name="fac_sb")
+        nc.scalar.copy(fac_sb[:], fac_t[:, :, FAC_AT])
 
         scores = [ps.tile([P, 2, M], F32, name="scores%d" % g, tag="scores%d" % g) for g in range(2)]
         for t in range(PACK):
             nc.tensor.matmul_mx(
                 out=scores[t // 2][:, t % 2, :],
                 lhsT=word_dealt[:, t, :].bitcast(FP4X4),
-                lhsT_scale=byte_dealt[:, t, :],
-                rhs=cent_mx[0][:].bitcast(FP8X4),
-                rhs_scale=cent_mx[1][:],
+                lhsT_scale=key_plane[:, t, :],
+                rhs=cent_codes[:].bitcast(FP8X4),
+                rhs_scale=cent_plane[:],
                 start=True,
                 stop=True,
             )
 
-        fac_t = ps.tile([P, PACK, P], F32, name="fac_t", tag="z3_1")
-        for t in range(PACK):
-            nc.tensor.transpose(fac_t[:, t, :], fac_rows[:, t:I:PACK], ident[:])
-        fac_sb = sb.tile([P, PACK], F32, name="fac_sb")
-        nc.scalar.copy(fac_sb[:], fac_t[:, :, 0])
-
-        def gather_and_turn(b):
-            listed = sb.tile([P, I], BF16, name="listed%d" % b, tag="listed%d" % b, align_bytes=64)
+        def gather(b):
+            listed = sb.tile([P, I], BF16, name="listed%d" % b, align_bytes=64)
             split = SPLITS[b]
             if split > 0:
                 nc.vector.tensor_copy(listed[:, :split], val_pool[b][:].indirect(offsets[:, : split // 16]))
             if split < I:
                 nc.scalar.activation(listed[:, split:], val_pool[b][:].indirect(offsets[:, split // 16 :]), ACT.Copy)
+            return listed
+
+        def turn(listed, name, bank):
             pairs = listed[:].bitcast(F32)
-            turned = ps.tile([P, 2, P], F32, name="turned%d" % b, tag="turned%d" % (b % 3))
+            turned = ps.tile([P, 2, P], F32, name=name, tag=bank)
             for u in range(2):
                 nc.tensor.transpose(turned[:, u, :], pairs[:, u : 2 * P : 2], ident[:])
             return turned
 
-        def weave(turned, rows):
-            nc.scalar.copy(
+        def weave(copy, turned, rows):
+            copy(
                 rows.bitcast(F32).rearrange("p (e u) -> p e u", u=2),
-                turned[:].rearrange("p u e -> p e u"),
+                turned.rearrange("p u e -> p e u"),
             )
 
-        def multiply(z, weights, moving):
+        def multiply(z, moving_codes, moving_plane):
             nc.tensor.matmul_mx(
                 out=z,
-                lhsT=weights[0][:].bitcast(FP8X4),
-                lhsT_scale=weights[1][:],
-                rhs=moving[0][:].bitcast(FP8X4),
-                rhs_scale=moving[1][:],
+                lhsT=w_codes[:].bitcast(FP8X4),
+                lhsT_scale=w_plane[:],
+                rhs=moving_codes.bitcast(FP8X4),
+                rhs_scale=moving_plane,
                 start=True,
                 stop=True,
             )
 
-        rows01 = sb.tile([P, 2 * I], BF16, name="rows01", align_bytes=64)
-
-        turned0 = gather_and_turn(0)
-        neg_max = behind(0, 0, [P, PACK], F32, "neg_max")
+        listed0 = gather(0)
+        neg_max = sb.tile([P, PACK], F32, name="neg_max")
         for g in range(2):
             nc.vector.tensor_reduce(neg_max[:, 2 * g : 2 * g + 2], scores[g][:], axis=AXIS.X, op=ALU.max, negate=True)
         expd = sb.tile([P, PACK, M], F32, name="expd")
@@ -149,8 +159,13 @@ def tile_attend_clustermeans_kernel(tc, pts_words, pts_scales, cent, fac, vals, 
                 expd[:, t, :], scores[t // 2][:, t % 2, :], ACT.Exp,
                 bias=neg_max[:, t : t + 1], accum_out=row_sum[:, t : t + 1],
             )
-        turned1 = gather_and_turn(1)
-        weave(turned0, rows01[:, :I])
+        def behind(b, at, shape, dtype, name):
+            return big.tile(shape, dtype, name=name, offset=b * ROW + at, align_bytes=64)
+
+        rows01 = sb.tile([P, 2 * I], BF16, name="rows01", align_bytes=64)
+        turned0 = turn(listed0, "turned0", "scores0")
+        turned1 = turn(gather(1), "turned1", "turn_a")
+        weave(nc.scalar.copy, turned0[:], rows01[:, :I])
         row_inv = behind(1, 0, [P, PACK], F32, "row_inv")
         nc.vector.reciprocal(row_inv[:], row_sum[:])
         factor = sb.tile([P, PACK], F32, name="factor")
@@ -164,50 +179,49 @@ def tile_attend_clustermeans_kernel(tc, pts_words, pts_scales, cent, fac, vals, 
             factor[:].unsqueeze(1).unsqueeze(3).to_broadcast([P, M // PACK, PACK, PACK]),
             ALU.mult,
         )
-        weave(turned1, rows01[:, I:])
-        share_t = ps.tile([P, P], F32, name="share_t", tag="turned1")
+        weave(nc.scalar.copy, turned1[:], rows01[:, I:])
+        share_t = ps.tile([P, P], F32, name="share_t", tag="turn_a")
         for t in range(PACK):
             nc.tensor.matmul(
                 share_t[:], share[:, t, :], ident[:],
                 start=(t == 0), stop=(t == PACK - 1), is_transpose=True,
             )
-
-        v01 = quantise("v01", rows01[:], sb.tile([P, 2 * P], U32, name="v01_codes", align_bytes=64))
-        w_mx = quantise("w", rows_w[:], sb.tile([P, P], U32, name="w_codes", align_bytes=64))
-        turned2 = gather_and_turn(2)
+        v01_codes, v01_plane = mx_tiles("v01", 2 * P)
+        quantise("v01", rows01[:], v01_codes[:], v01_plane[:])
+        w_codes, w_plane = mx_tiles("w", P)
+        quantise("w", rows_w[:], w_codes[:], w_plane[:])
+        turned2 = turn(gather(2), "turned2", "turn_b")
         col_sum = sb.tile([P, 1], F32, name="col_sum")
         nc.vector.tensor_reduce(col_sum[:], share_t[:], axis=AXIS.X, op=ALU.add)
         col_inv = sb.tile([P, 1], F32, name="col_inv")
         nc.vector.reciprocal(col_inv[:], col_sum[:])
         z01 = ps.tile([P, 2 * P], F32, name="z01")
-        multiply(z01[:], w_mx, v01)
-        turned3 = gather_and_turn(3)
+        multiply(z01[:], v01_codes[:], v01_plane[:])
+        turned3 = turn(gather(3), "turned3", "turn_c")
         rows2 = behind(3, 4096, [P, I], BF16, "rows2")
-        weave(turned2, rows2[:])
+        weave(nc.scalar.copy, turned2[:], rows2[:])
         mean01 = behind(3, 1024, [P, 2 * P], F32, "mean01")
         nc.vector.tensor_scalar_mul(mean01[:], z01[:], col_inv[:])
         nc.sync.dma_start(out[:, : 2 * P], mean01[:])
-        v2 = quantise("v2", rows2[:], sb.tile([P, P], U32, name="v2_codes", align_bytes=64))
+        v2_codes, v2_plane = mx_tiles("v2", P)
+        quantise("v2", rows2[:], v2_codes[:], v2_plane[:])
         halves = []
         for h in range(2):
             rows_h = sb.tile([P, I // 2], BF16, name="rows3_%d" % h, align_bytes=64)
-            nc.scalar.copy(
-                rows_h[:].bitcast(F32).rearrange("p (e u) -> p e u", u=2),
-                turned3[:, :, h * HALF : (h + 1) * HALF].rearrange("p u e -> p e u"),
-            )
+            weave(nc.scalar.copy, turned3[:, :, h * HALF : (h + 1) * HALF], rows_h[:])
             halves.append(rows_h)
         v3 = []
         for h in range(2):
-            codes_h = sb.tile([P, HALF], U32, name="v3_codes%d" % h, align_bytes=64)
-            v3.append(quantise("v3_%d" % h, halves[h][:], codes_h))
+            codes_h, plane_h = mx_tiles("v3_%d" % h, HALF)
+            v3.append(quantise("v3", halves[h][:], codes_h[:], plane_h[:]))
         z2 = ps.tile([P, P], F32, name="z2", tag="scores1")
-        multiply(z2[:], w_mx, v2)
+        multiply(z2[:], v2_codes[:], v2_plane[:])
         mean2 = sb.tile([P, P], F32, name="mean2")
         nc.vector.tensor_scalar_mul(mean2[:], z2[:], col_inv[:])
         nc.sync.dma_start(out[:, 2 * P : 3 * P], mean2[:])
         mean3 = sb.tile([P, P], F32, name="mean3")
         for h in range(2):
             z_h = ps.tile([P, HALF], F32, name="z3_%d" % h, tag="z3_%d" % h)
-            multiply(z_h[:], w_mx, v3[h])
+            multiply(z_h[:], v3[h][0], v3[h][1])
             nc.scalar.activation(mean3[:, h * HALF : (h + 1) * HALF], z_h[:], ACT.Copy, scale=col_inv[:])
         nc.sync.dma_start(out[:, 3 * P :], mean3[:])

@@ -25,7 +25,7 @@ ROW = 4 * T
 HALF = P // 2
 RUN = 8
 SCALE_ROWS = D // 32
-SCALE_AT = 16
+SCALE_AT = P - SCALE_ROWS
 FAC_AT = 4
 SPLITS = (320, 384, 0, 288)
 
@@ -41,8 +41,7 @@ def tile_attend_clustermeans_kernel(tc, pts_words, pts_scales, cent, fac, vals, 
         nc.sync.dma_start(offsets[:], offs)
         byte_pool = big.tile([P, T], U8, name="byte_pool", offset=2 * ROW - T // 2, align_bytes=64)
         nc.scalar.dma_start(byte_pool[SCALE_AT : SCALE_AT + SCALE_ROWS, :].bitcast(I32), pts_scales[0].bitcast(I32))
-        for lo, hi in ((0, SCALE_AT), (32, 64), (64, P)):
-            nc.vector.memset(byte_pool[lo:hi, :].bitcast(I32), 0)
+        nc.vector.memset(byte_pool[:SCALE_AT, :].bitcast(I32), 0)
         word_pool = big.tile([P, T], U16, name="word_pool", offset=3 * ROW, align_bytes=64)
         nc.sync.dma_start(word_pool[:].bitcast(I32), pts_words[0].bitcast(I32))
         cent_raw = sb.tile([P, PACK, M], F32, name="cent_raw", align_bytes=64)
@@ -162,16 +161,17 @@ def tile_attend_clustermeans_kernel(tc, pts_words, pts_scales, cent, fac, vals, 
         def behind(b, at, shape, dtype, name):
             return big.tile(shape, dtype, name=name, offset=b * ROW + at, align_bytes=64)
 
-        rows01 = sb.tile([P, 2 * I], BF16, name="rows01", align_bytes=64)
         turned0 = turn(listed0, "turned0", "scores0")
         turned1 = turn(gather(1), "turned1", "turn_a")
+        rows01 = behind(1, 1024, [P, 2 * I], BF16, "rows01")
         weave(nc.scalar.copy, turned0[:], rows01[:, :I])
         row_inv = behind(1, 0, [P, PACK], F32, "row_inv")
         nc.vector.reciprocal(row_inv[:], row_sum[:])
         factor = sb.tile([P, PACK], F32, name="factor")
         nc.vector.tensor_tensor(factor[:], row_inv[:], fac_sb[:], ALU.mult)
         share = sb.tile([P, PACK, M], F32, name="share")
-        nc.vector.tensor_tensor(share[:], expd[:], row_inv[:].unsqueeze(2).to_broadcast([P, PACK, M]), ALU.mult)
+        for t in range(PACK):
+            nc.vector.tensor_scalar_mul(share[:, t, :], expd[:, t, :], row_inv[:, t : t + 1])
         rows_w = sb.tile([P, I], BF16, name="rows_w", align_bytes=64)
         nc.vector.tensor_tensor(
             rows_w[:].rearrange("p (c i t) -> p c t i", i=PACK, t=PACK),
@@ -193,11 +193,11 @@ def tile_attend_clustermeans_kernel(tc, pts_words, pts_scales, cent, fac, vals, 
         turned2 = turn(gather(2), "turned2", "turn_b")
         col_sum = sb.tile([P, 1], F32, name="col_sum")
         nc.vector.tensor_reduce(col_sum[:], share_t[:], axis=AXIS.X, op=ALU.add)
-        col_inv = sb.tile([P, 1], F32, name="col_inv")
-        nc.vector.reciprocal(col_inv[:], col_sum[:])
         z01 = ps.tile([P, 2 * P], F32, name="z01")
         multiply(z01[:], v01_codes[:], v01_plane[:])
         turned3 = turn(gather(3), "turned3", "turn_c")
+        col_inv = behind(3, 0, [P, 1], F32, "col_inv")
+        nc.vector.reciprocal(col_inv[:], col_sum[:])
         rows2 = behind(3, 4096, [P, I], BF16, "rows2")
         weave(nc.scalar.copy, turned2[:], rows2[:])
         mean01 = behind(3, 1024, [P, 2 * P], F32, "mean01")

@@ -27,7 +27,7 @@ RUN = 8
 SCALE_ROWS = D // 32
 SCALE_AT = P - SCALE_ROWS
 FAC_AT = 4
-SPLITS = (320, 384, 0, 288)
+SPLITS = (320, 320, 128, 256)
 
 
 def tile_attend_clustermeans_kernel(tc, pts_words, pts_scales, cent, fac, vals, offs, out):
@@ -180,7 +180,7 @@ def tile_attend_clustermeans_kernel(tc, pts_words, pts_scales, cent, fac, vals, 
             ALU.mult,
         )
         weave(nc.scalar.copy, turned1[:], rows01[:, I:])
-        share_t = ps.tile([P, P], F32, name="share_t", tag="turn_a")
+        share_t = ps.tile([P, P], F32, name="share_t", tag="z3_1")
         for t in range(PACK):
             nc.tensor.matmul(
                 share_t[:], share[:, t, :], ident[:],

@@ -26,7 +26,7 @@ HALF = P // 2
 RUN = 8
 SCALE_ROWS = D // 32
 SCALE_AT = P - SCALE_ROWS
-FAC_AT = 4
+FAC_AT = HALF - 1
 SPLITS = (320, 320, 128, 256)
 
 
@@ -47,8 +47,11 @@ def tile_attend_clustermeans_kernel(tc, pts_words, pts_scales, cent, fac, vals, 
         cent_raw = sb.tile([P, PACK, M], F32, name="cent_raw", align_bytes=64)
         nc.sync.dma_start(cent_raw[:], cent.rearrange("(p t) m -> p t m", t=PACK))
         fac_rows = sb.tile([P, I], F32, name="fac_rows")
-        nc.vector.memset(fac_rows[:], 0.0)
         nc.sync.dma_start(fac_rows[FAC_AT : FAC_AT + 1, :], fac.rearrange("i o -> o i"))
+        zero = sb.tile([P, 1], F32, name="zero")
+        nc.vector.memset(zero[:], 0.0)
+        nc.scalar.copy(fac_rows[:FAC_AT, :], zero[:FAC_AT, :].to_broadcast([FAC_AT, I]))
+        nc.vector.memset(fac_rows[HALF:, :], 0.0)
         key_plane = sb.tile([P, PACK, P], U8, name="key_plane", align_bytes=64)
         plane_words = key_plane[:].rearrange("p t s -> p (t s)").bitcast(I32)
         nc.vector.memset(plane_words, 0)
@@ -68,7 +71,8 @@ def tile_attend_clustermeans_kernel(tc, pts_words, pts_scales, cent, fac, vals, 
         nc.vector.tensor_copy(byte_dealt[:].rearrange("p t s -> p s t"), byte_pool[:].indirect(offsets[:]))
         dealt_words = byte_dealt[:].rearrange("p t s -> p (t s)").bitcast(I32)
         for r in range(4):
-            nc.sync.dma_start(plane_words[r:P:32, :], dealt_words[SCALE_AT + r : SCALE_AT + SCALE_ROWS : 4, :])
+            queue = nc.scalar if r == 0 else nc.sync
+            queue.dma_start(plane_words[r:P:32, :], dealt_words[SCALE_AT + r : SCALE_AT + SCALE_ROWS : 4, :])
         word_list = sb.tile([P, I], U16, name="word_list", align_bytes=64)
         nc.vector.tensor_copy(word_list[:], word_pool[:].indirect(offsets[:]))
         for b in range(1, BLOCKS):
@@ -165,11 +169,11 @@ def tile_attend_clustermeans_kernel(tc, pts_words, pts_scales, cent, fac, vals, 
         turned1 = turn(gather(1), "turned1", "turn_a")
         rows01 = behind(1, 1024, [P, 2 * I], BF16, "rows01")
         weave(nc.scalar.copy, turned0[:], rows01[:, :I])
-        row_inv = behind(1, 0, [P, PACK], F32, "row_inv")
+        row_inv = sb.tile([P, PACK], F32, name="row_inv")
         nc.vector.reciprocal(row_inv[:], row_sum[:])
-        factor = sb.tile([P, PACK], F32, name="factor")
+        factor = behind(1, 0, [P, PACK], F32, "factor")
         nc.vector.tensor_tensor(factor[:], row_inv[:], fac_sb[:], ALU.mult)
-        share = sb.tile([P, PACK, M], F32, name="share")
+        share = behind(1, 4096, [P, PACK, M], F32, "share")
         for t in range(PACK):
             nc.vector.tensor_scalar_mul(share[:, t, :], expd[:, t, :], row_inv[:, t : t + 1])
         rows_w = sb.tile([P, I], BF16, name="rows_w", align_bytes=64)

@@ -71,7 +71,7 @@ def tile_attend_clustermeans_kernel(tc, pts_words, pts_scales, cent, fac, vals, 
         nc.vector.tensor_copy(byte_dealt[:].rearrange("p t s -> p s t"), byte_pool[:].indirect(offsets[:]))
         dealt_words = byte_dealt[:].rearrange("p t s -> p (t s)").bitcast(I32)
         for r in range(4):
-            queue = nc.scalar if r == 0 else nc.sync
+            queue = nc.scalar if r % 2 == 0 else nc.sync
             queue.dma_start(plane_words[r:P:32, :], dealt_words[SCALE_AT + r : SCALE_AT + SCALE_ROWS : 4, :])
         word_list = sb.tile([P, I], U16, name="word_list", align_bytes=64)
         nc.vector.tensor_copy(word_list[:], word_pool[:].indirect(offsets[:]))

@@ -22,12 +22,13 @@ P = 128
 PACK = 4
 BLOCKS = E // P
 ROW = 4 * T
+AUX = BLOCKS * ROW
 HALF = P // 2
 RUN = 8
 SCALE_ROWS = D // 32
 SCALE_AT = P - SCALE_ROWS
 FAC_AT = HALF - 1
-SPLITS = (320, 320, 128, 256)
+SPLITS = (320, 320, 0, 256)
 
 
 def tile_attend_clustermeans_kernel(tc, pts_words, pts_scales, cent, fac, vals, offs, out):
@@ -39,10 +40,10 @@ def tile_attend_clustermeans_kernel(tc, pts_words, pts_scales, cent, fac, vals, 
 
         offsets = sb.tile([P, I // 16], U16, name="offsets")
         nc.sync.dma_start(offsets[:], offs)
-        byte_pool = big.tile([P, T], U8, name="byte_pool", offset=2 * ROW - T // 2, align_bytes=64)
+        byte_pool = big.tile([P, T], U8, name="byte_pool", offset=ROW, align_bytes=64)
         nc.scalar.dma_start(byte_pool[SCALE_AT : SCALE_AT + SCALE_ROWS, :].bitcast(I32), pts_scales[0].bitcast(I32))
         nc.vector.memset(byte_pool[:SCALE_AT, :].bitcast(I32), 0)
-        word_pool = big.tile([P, T], U16, name="word_pool", offset=3 * ROW, align_bytes=64)
+        word_pool = big.tile([P, T], U16, name="word_pool", offset=2 * ROW, align_bytes=64)
         nc.sync.dma_start(word_pool[:].bitcast(I32), pts_words[0].bitcast(I32))
         cent_raw = sb.tile([P, PACK, M], F32, name="cent_raw", align_bytes=64)
         nc.sync.dma_start(cent_raw[:], cent.rearrange("(p t) m -> p t m", t=PACK))
@@ -62,7 +63,8 @@ def tile_attend_clustermeans_kernel(tc, pts_words, pts_scales, cent, fac, vals, 
 
         def load_block(b):
             tile_b = big.tile([P, T], F32, name="val_pool%d" % b, offset=b * ROW, align_bytes=64)
-            nc.sync.dma_start(tile_b[:], vals[b * P : (b + 1) * P, :])
+            queue = nc.scalar if b % 2 == 1 else nc.sync
+            queue.dma_start(tile_b[:], vals[b * P : (b + 1) * P, :])
             val_pool.append(tile_b)
 
         load_block(0)
@@ -73,9 +75,9 @@ def tile_attend_clustermeans_kernel(tc, pts_words, pts_scales, cent, fac, vals, 
         for r in range(4):
             queue = nc.scalar if r % 2 == 0 else nc.sync
             queue.dma_start(plane_words[r:P:32, :], dealt_words[SCALE_AT + r : SCALE_AT + SCALE_ROWS : 4, :])
-        word_list = sb.tile([P, I], U16, name="word_list", align_bytes=64)
+        word_list = big.tile([P, I], U16, name="word_list", offset=AUX + 2 * I, align_bytes=64)
         nc.vector.tensor_copy(word_list[:], word_pool[:].indirect(offsets[:]))
-        for b in range(1, BLOCKS):
+        for b in range(1, BLOCKS - 1):
             load_block(b)
 
         def quantise(name, rows, codes, plane):
@@ -87,7 +89,7 @@ def tile_attend_clustermeans_kernel(tc, pts_words, pts_scales, cent, fac, vals, 
             plane = sb.tile([P, width], U8, name=name + "_bytes", align_bytes=64)
             return codes, plane
 
-        cent_bf = sb.tile([P, M, PACK], BF16, name="cent_bf", align_bytes=64)
+        cent_bf = big.tile([P, M, PACK], BF16, name="cent_bf", offset=AUX, align_bytes=64)
         nc.scalar.copy(
             cent_bf[:].rearrange("p (c i) t -> p c t i", i=PACK),
             cent_raw[:].rearrange("p t (c i) -> p c t i", i=PACK),
@@ -119,7 +121,12 @@ def tile_attend_clustermeans_kernel(tc, pts_words, pts_scales, cent, fac, vals, 
             )
 
         def gather(b):
-            listed = sb.tile([P, I], BF16, name="listed%d" % b, align_bytes=64)
+            if b == 0:
+                listed = big.tile([P, I], BF16, name="listed0", offset=AUX + I, align_bytes=64)
+            elif b < 3:
+                listed = big.tile([P, I], BF16, name="listed%d" % b, offset=AUX + 4 * I, align_bytes=64)
+            else:
+                listed = sb.tile([P, I], BF16, name="listed3", align_bytes=64)
             split = SPLITS[b]
             if split > 0:
                 nc.vector.tensor_copy(listed[:, :split], val_pool[b][:].indirect(offsets[:, : split // 16]))
@@ -152,16 +159,20 @@ def tile_attend_clustermeans_kernel(tc, pts_words, pts_scales, cent, fac, vals, 
             )
 
         listed0 = gather(0)
-        neg_max = sb.tile([P, PACK], F32, name="neg_max")
-        for g in range(2):
-            nc.vector.tensor_reduce(neg_max[:, 2 * g : 2 * g + 2], scores[g][:], axis=AXIS.X, op=ALU.max, negate=True)
+        neg_max = []
+        for g, at in enumerate((AUX + 4 * I, 3 * ROW)):
+            max_g = big.tile([P, 2], F32, name="neg_max%d" % g, offset=at, align_bytes=64)
+            nc.vector.tensor_reduce(max_g[:], scores[g][:], axis=AXIS.X, op=ALU.max, negate=True)
+            neg_max.append(max_g)
         expd = sb.tile([P, PACK, M], F32, name="expd")
         row_sum = sb.tile([P, PACK], F32, name="row_sum")
         for t in range(PACK):
             nc.scalar.activation(
                 expd[:, t, :], scores[t // 2][:, t % 2, :], ACT.Exp,
-                bias=neg_max[:, t : t + 1], accum_out=row_sum[:, t : t + 1],
+                bias=neg_max[t // 2][:, t % 2 : t % 2 + 1], accum_out=row_sum[:, t : t + 1],
             )
+        load_block(BLOCKS - 1)
+
         def behind(b, at, shape, dtype, name):
             return big.tile(shape, dtype, name=name, offset=b * ROW + at, align_bytes=64)
 

@@ -48,7 +48,7 @@ def tile_attend_clustermeans_kernel(tc, pts_words, pts_scales, cent, fac, vals, 
         cent_raw = sb.tile([P, PACK, M], F32, name="cent_raw", align_bytes=64)
         nc.sync.dma_start(cent_raw[:], cent.rearrange("(p t) m -> p t m", t=PACK))
         fac_rows = sb.tile([P, I], F32, name="fac_rows")
-        nc.sync.dma_start(fac_rows[FAC_AT : FAC_AT + 1, :], fac.rearrange("i o -> o i"))
+        nc.scalar.dma_start(fac_rows[FAC_AT : FAC_AT + 1, :], fac.rearrange("i o -> o i"))
         zero = sb.tile([P, 1], F32, name="zero")
         nc.vector.memset(zero[:], 0.0)
         nc.scalar.copy(fac_rows[:FAC_AT, :], zero[:FAC_AT, :].to_broadcast([FAC_AT, I]))

from contextlib import ExitStack

import concourse.mybir as mybir
from concourse.masks import make_identity

D, T, I, M, E = 512, 2048, 512, 128, 512
FLOPS = 2 * I * D * M + 2 * M * I * E

F32 = mybir.dt.float32
BF16 = mybir.dt.bfloat16
I32 = mybir.dt.int32
U32 = mybir.dt.uint32
U16 = mybir.dt.uint16
U8 = mybir.dt.uint8
FP8X4 = mybir.dt.float8_e4m3fn_x4
FP4X4 = mybir.dt.float4_e2m1fn_x4
ALU = mybir.AluOpType
ACT = mybir.ActivationFunctionType
AXIS = mybir.AxisListType

P = 128
PACK = 4
BLOCKS = E // P
ROW = 4 * T
AUX = BLOCKS * ROW
HALF = P // 2
RUN = 8
SCALE_ROWS = D // 32
SCALE_AT = P - SCALE_ROWS
FAC_AT = HALF - 1
SPLITS = (320, 320, 0, 256)


def tile_attend_clustermeans_kernel(tc, pts_words, pts_scales, cent, fac, vals, offs, out):
    nc = tc.nc
    with ExitStack() as ctx:
        sb = ctx.enter_context(tc.tile_pool(name="sb", bufs=1))
        big = ctx.enter_context(tc.tile_pool(name="big", bufs=1))
        ps = ctx.enter_context(tc.psum_pool(name="ps", bufs=1))

        offsets = sb.tile([P, I // 16], U16, name="offsets")
        nc.sync.dma_start(offsets[:], offs)
        byte_pool = big.tile([P, T], U8, name="byte_pool", offset=ROW, align_bytes=64)
        nc.scalar.dma_start(byte_pool[SCALE_AT : SCALE_AT + SCALE_ROWS, :].bitcast(I32), pts_scales[0].bitcast(I32))
        nc.vector.memset(byte_pool[:SCALE_AT, :].bitcast(I32), 0)
        word_pool = big.tile([P, T], U16, name="word_pool", offset=2 * ROW, align_bytes=64)
        nc.sync.dma_start(word_pool[:].bitcast(I32), pts_words[0].bitcast(I32))
        cent_raw = sb.tile([P, PACK, M], F32, name="cent_raw", align_bytes=64)
        nc.sync.dma_start(cent_raw[:], cent.rearrange("(p t) m -> p t m", t=PACK))
        fac_rows = sb.tile([P, I], F32, name="fac_rows")
        nc.scalar.dma_start(fac_rows[FAC_AT : FAC_AT + 1, :], fac.rearrange("i o -> o i"))
        zero = sb.tile([P, 1], F32, name="zero")
        nc.vector.memset(zero[:], 0.0)
        nc.scalar.copy(fac_rows[:FAC_AT, :], zero[:FAC_AT, :].to_broadcast([FAC_AT, I]))
        nc.vector.memset(fac_rows[HALF:, :], 0.0)
        key_plane = sb.tile([P, PACK, P], U8, name="key_plane", align_bytes=64)
        plane_words = key_plane[:].rearrange("p t s -> p (t s)").bitcast(I32)
        nc.vector.memset(plane_words, 0)
        ident = sb.tile([P, P], F32, name="ident")
        make_identity(nc, ident[:])

        val_pool = []

        def load_block(b):
            tile_b = big.tile([P, T], F32, name="val_pool%d" % b, offset=b * ROW, align_bytes=64)
            queue = nc.scalar if b % 2 == 1 else nc.sync
            queue.dma_start(tile_b[:], vals[b * P : (b + 1) * P, :])
            val_pool.append(tile_b)

        load_block(0)

        byte_dealt = sb.tile([P, PACK, P], U8, name="byte_dealt", align_bytes=64)
        nc.vector.tensor_copy(byte_dealt[:].rearrange("p t s -> p s t"), byte_pool[:].indirect(offsets[:]))
        dealt_words = byte_dealt[:].rearrange("p t s -> p (t s)").bitcast(I32)
        for r in range(4):
            queue = nc.scalar if r % 2 == 0 else nc.sync
            queue.dma_start(plane_words[r:P:32, :], dealt_words[SCALE_AT + r : SCALE_AT + SCALE_ROWS : 4, :])
        word_list = big.tile([P, I], U16, name="word_list", offset=AUX + 2 * I, align_bytes=64)
        nc.vector.tensor_copy(word_list[:], word_pool[:].indirect(offsets[:]))
        for b in range(1, BLOCKS - 1):
            load_block(b)

        def quantise(name, rows, codes, plane):
            nc.vector.quantize_mx(out=codes.bitcast(FP8X4), scales=plane, in_=rows)
            return codes, plane

        def mx_tiles(name, width):
            codes = sb.tile([P, width], U32, name=name + "_codes", align_bytes=64)
            plane = sb.tile([P, width], U8, name=name + "_bytes", align_bytes=64)
            return codes, plane

        cent_bf = big.tile([P, M, PACK], BF16, name="cent_bf", offset=AUX, align_bytes=64)
        nc.scalar.copy(
            cent_bf[:].rearrange("p (c i) t -> p c t i", i=PACK),
            cent_raw[:].rearrange("p t (c i) -> p c t i", i=PACK),
        )
        word_dealt = sb.tile([P, PACK, P], U16, name="word_dealt", align_bytes=64)
        nc.vector.tensor_copy(
            word_dealt[:].rearrange("p t (c i) -> p c t i", i=RUN),
            word_list[:].rearrange("p (c i t) -> p c t i", t=PACK, i=RUN),
        )
        cent_codes, cent_plane = mx_tiles("cent", M)
        quantise("cent", cent_bf[:].rearrange("p m t -> p (m t)"), cent_codes[:], cent_plane[:])

        fac_t = ps.tile([P, PACK, P], F32, name="fac_t", tag="turn_a")
        for t in range(PACK):
            nc.tensor.transpose(fac_t[:, t, :], fac_rows[:, t:I:PACK], ident[:])
        fac_sb = sb.tile([P, PACK], F32, name="fac_sb")
        nc.scalar.copy(fac_sb[:], fac_t[:, :, FAC_AT])

        scores = [ps.tile([P, 2, M], F32, name="scores%d" % g, tag="scores%d" % g) for g in range(2)]
        for t in range(PACK):
            nc.tensor.matmul_mx(
                out=scores[t // 2][:, t % 2, :],
                lhsT=word_dealt[:, t, :].bitcast(FP4X4),
                lhsT_scale=key_plane[:, t, :],
                rhs=cent_codes[:].bitcast(FP8X4),
                rhs_scale=cent_plane[:],
                start=True,
                stop=True,
            )

        def gather(b):
            if b == 0:
                listed = big.tile([P, I], BF16, name="listed0", offset=AUX + I, align_bytes=64)
            elif b < 3:
                listed = big.tile([P, I], BF16, name="listed%d" % b, offset=AUX + 4 * I, align_bytes=64)
            else:
                listed = sb.tile([P, I], BF16, name="listed3", align_bytes=64)
            split = SPLITS[b]
            if split > 0:
                nc.vector.tensor_copy(listed[:, :split], val_pool[b][:].indirect(offsets[:, : split // 16]))
            if split < I:
                nc.scalar.activation(listed[:, split:], val_pool[b][:].indirect(offsets[:, split // 16 :]), ACT.Copy)
            return listed

        def turn(listed, name, bank):
            pairs = listed[:].bitcast(F32)
            turned = ps.tile([P, 2, P], F32, name=name, tag=bank)
            for u in range(2):
                nc.tensor.transpose(turned[:, u, :], pairs[:, u : 2 * P : 2], ident[:])
            return turned

        def weave(copy, turned, rows):
            copy(
                rows.bitcast(F32).rearrange("p (e u) -> p e u", u=2),
                turned.rearrange("p u e -> p e u"),
            )

        def multiply(z, moving_codes, moving_plane):
            nc.tensor.matmul_mx(
                out=z,
                lhsT=w_codes[:].bitcast(FP8X4),
                lhsT_scale=w_plane[:],
                rhs=moving_codes.bitcast(FP8X4),
                rhs_scale=moving_plane,
                start=True,
                stop=True,
            )

        listed0 = gather(0)
        neg_max = []
        for g, at in enumerate((AUX + 4 * I, 3 * ROW)):
            max_g = big.tile([P, 2], F32, name="neg_max%d" % g, offset=at, align_bytes=64)
            nc.vector.tensor_reduce(max_g[:], scores[g][:], axis=AXIS.X, op=ALU.max, negate=True)
            neg_max.append(max_g)
        expd = sb.tile([P, PACK, M], F32, name="expd")
        row_sum = sb.tile([P, PACK], F32, name="row_sum")
        for t in range(PACK):
            nc.scalar.activation(
                expd[:, t, :], scores[t // 2][:, t % 2, :], ACT.Exp,
                bias=neg_max[t // 2][:, t % 2 : t % 2 + 1], accum_out=row_sum[:, t : t + 1],
            )
        load_block(BLOCKS - 1)

        def behind(b, at, shape, dtype, name):
            return big.tile(shape, dtype, name=name, offset=b * ROW + at, align_bytes=64)

        turned0 = turn(listed0, "turned0", "scores0")
        turned1 = turn(gather(1), "turned1", "turn_a")
        rows01 = behind(1, 1024, [P, 2 * I], BF16, "rows01")
        weave(nc.scalar.copy, turned0[:], rows01[:, :I])
        row_inv = sb.tile([P, PACK], F32, name="row_inv")
        nc.vector.reciprocal(row_inv[:], row_sum[:])
        factor = behind(1, 0, [P, PACK], F32, "factor")
        nc.vector.tensor_tensor(factor[:], row_inv[:], fac_sb[:], ALU.mult)
        share = behind(1, 4096, [P, PACK, M], F32, "share")
        for t in range(PACK):
            nc.vector.tensor_scalar_mul(share[:, t, :], expd[:, t, :], row_inv[:, t : t + 1])
        rows_w = sb.tile([P, I], BF16, name="rows_w", align_bytes=64)
        nc.vector.tensor_tensor(
            rows_w[:].rearrange("p (c i t) -> p c t i", i=PACK, t=PACK),
            expd[:].rearrange("p t (c i) -> p c t i", i=PACK),
            factor[:].unsqueeze(1).unsqueeze(3).to_broadcast([P, M // PACK, PACK, PACK]),
            ALU.mult,
        )
        weave(nc.scalar.copy, turned1[:], rows01[:, I:])
        share_t = ps.tile([P, P], F32, name="share_t", tag="z3_1")
        for t in range(PACK):
            nc.tensor.matmul(
                share_t[:], share[:, t, :], ident[:],
                start=(t == 0), stop=(t == PACK - 1), is_transpose=True,
            )
        v01_codes, v01_plane = mx_tiles("v01", 2 * P)
        quantise("v01", rows01[:], v01_codes[:], v01_plane[:])
        w_codes, w_plane = mx_tiles("w", P)
        quantise("w", rows_w[:], w_codes[:], w_plane[:])
        turned2 = turn(gather(2), "turned2", "turn_b")
        col_sum = sb.tile([P, 1], F32, name="col_sum")
        nc.vector.tensor_reduce(col_sum[:], share_t[:], axis=AXIS.X, op=ALU.add)
        z01 = ps.tile([P, 2 * P], F32, name="z01")
        multiply(z01[:], v01_codes[:], v01_plane[:])
        turned3 = turn(gather(3), "turned3", "turn_c")
        col_inv = behind(3, 0, [P, 1], F32, "col_inv")
        nc.vector.reciprocal(col_inv[:], col_sum[:])
        rows2 = behind(3, 4096, [P, I], BF16, "rows2")
        weave(nc.scalar.copy, turned2[:], rows2[:])
        mean01 = behind(3, 1024, [P, 2 * P], F32, "mean01")
        nc.vector.tensor_scalar_mul(mean01[:], z01[:], col_inv[:])
        nc.sync.dma_start(out[:, : 2 * P], mean01[:])
        v2_codes, v2_plane = mx_tiles("v2", P)
        quantise("v2", rows2[:], v2_codes[:], v2_plane[:])
        halves = []
        for h in range(2):
            rows_h = sb.tile([P, I // 2], BF16, name="rows3_%d" % h, align_bytes=64)
            weave(nc.scalar.copy, turned3[:, :, h * HALF : (h + 1) * HALF], rows_h[:])
            halves.append(rows_h)
        v3 = []
        for h in range(2):
            codes_h, plane_h = mx_tiles("v3_%d" % h, HALF)
            v3.append(quantise("v3", halves[h][:], codes_h[:], plane_h[:]))
        z2 = ps.tile([P, P], F32, name="z2", tag="scores1")
        multiply(z2[:], v2_codes[:], v2_plane[:])
        mean2 = sb.tile([P, P], F32, name="mean2")
        nc.vector.tensor_scalar_mul(mean2[:], z2[:], col_inv[:])
        nc.sync.dma_start(out[:, 2 * P : 3 * P], mean2[:])
        mean3 = sb.tile([P, P], F32, name="mean3")
        for h in range(2):
            z_h = ps.tile([P, HALF], F32, name="z3_%d" % h, tag="z3_%d" % h)
            multiply(z_h[:], v3[h][0], v3[h][1])
            nc.scalar.activation(mean3[:, h * HALF : (h + 1) * HALF], z_h[:], ACT.Copy, scale=col_inv[:])
        nc.sync.dma_start(out[:, 3 * P :], mean3[:])
